import numpy as np
import ml_dtypes


def mxq(x, axis, fmt="e4m3"):
    dtype, down = {"e4m3": (ml_dtypes.float8_e4m3fn, 7), "e5m2": (ml_dtypes.float8_e5m2, 14)}[fmt]
    v = np.moveaxis(np.asarray(x, np.float32).astype(ml_dtypes.bfloat16).astype(np.float64), axis, -1)
    blocks = v.reshape(v.shape[:-1] + (-1, 32))
    amax = np.abs(blocks).max(-1, keepdims=True)
    byte = np.maximum(np.where(amax > 0, np.frexp(amax)[1] - 1 + 127, 0) - down, 1)
    scale = np.exp2(byte - 127.0)
    codes = (blocks / scale).astype(np.float32).astype(dtype).astype(np.float64)
    return np.moveaxis((codes * scale).reshape(v.shape), -1, axis)


WIDE = False


def mx_kscale(k):
    if not WIDE:
        return np.ones(k)
    levels = np.array([10, -10, 5, -5, 0])
    if k % 512:
        return np.exp2(np.random.permutation(np.resize(levels, k // 32))).repeat(32)
    a = np.empty((k // 512, 16))
    for p in range(k // 512):
        a[p, :8] = np.random.permutation(np.resize(levels, 8))
        for g in range(8):
            far = levels[np.abs(levels - a[p, g]) >= 10]
            a[p, g + 8] = far[np.random.randint(len(far))]
    return np.exp2(a.ravel()).repeat(32)


def f64(x):
    return np.asarray(x).astype(np.float64)


def striped(idx):
    return np.tile(np.asarray(idx).reshape(-1, 16).T, (8, 1)).astype(np.uint16)


def unstriped(offs):
    return offs[:16].T.reshape(-1).astype(np.int64)


E2M1 = np.array([0.0, 0.5, 1.0, 1.5, 2.0, 3.0, 4.0, 6.0, -0.0, -0.5, -1.0, -1.5, -2.0, -3.0, -4.0, -6.0])


def pack_weight(w, fmt):
    k, n = w.shape
    w = f64(np.asarray(w, np.float32).astype(ml_dtypes.bfloat16)).reshape(k // 32, 32, n)
    amax = np.abs(w).max(1)
    if fmt == "e4m3":
        byte = np.frexp(amax)[1] - 1 + 127 - 7
    else:
        mant, ex = np.frexp(amax / 6.0)
        byte = np.where(mant > 0.5, ex, ex - 1) + 127
    byte = np.clip(np.where(amax > 0, byte, 1), 1, 254)
    scaled = (w * np.exp2(127.0 - byte)[:, None, :]).reshape(k, n).astype(np.float32)
    by_word = np.ascontiguousarray(scaled.reshape(k // 512, 128, 4, n).transpose(0, 1, 3, 2))
    if fmt == "e4m3":
        words = by_word.astype(ml_dtypes.float8_e4m3fn).view(np.uint8)
    else:
        c = by_word.astype(ml_dtypes.float4_e2m1fn).view(np.uint8) & 0xF
        words = (c[..., 0::2] | (c[..., 1::2] << 4)).reshape(k // 512, 128, 2 * n)
    return np.ascontiguousarray(words), np.ascontiguousarray(byte.astype(np.uint8).reshape(k // 512, 16, n))


def unpack_weight(words, scales, fmt):
    g, _, n = scales.shape
    words = np.ascontiguousarray(words).reshape(g, 128, n, -1)
    if fmt == "e4m3":
        vals = words.view(ml_dtypes.float8_e4m3fn).astype(np.float64)
    else:
        nib = np.empty((g, 128, n, 4), np.uint8)
        nib[..., 0::2] = words & 0xF
        nib[..., 1::2] = words >> 4
        vals = E2M1[nib]
    vals = vals * np.repeat(np.exp2(scales.astype(np.float64) - 127.0), 8, axis=1)[..., None]
    return vals.transpose(0, 1, 3, 2).reshape(g * 512, n)


B, N, T, D, DV, NQ = 2, 1024, 4096, 512, 256, 128
PAGE = 512


def setup_inputs():
    n = np.random.standard_normal
    pages = np.random.permutation(T // PAGE)[:B * N // PAGE]
    idx = (pages[:, None] * PAGE + np.arange(PAGE)[None, :]).reshape(-1)
    s = mx_kscale(D)[:, None]
    u = np.ones(T)
    u[idx] = mx_kscale(B * N)
    r = np.random.uniform(0.5, 2.0, T)
    k = n((D, T)) / s
    v = n((DV, T)) / (u * r)
    kp = pack_weight(k, "e4m3")
    vp = pack_weight(v.T, "e4m3")
    return {
        "qT": (n((B, D, NQ)) * s * (1.00 / np.sqrt(D))).astype(np.float32),
        "k_words": kp[0],
        "k_scales": kp[1],
        "v_words": vp[0],
        "v_scales": vp[1],
        "vs": np.tile(u * r, (128, 1)).astype(np.float32),
        "og": n((B, NQ, DV)).astype(np.float32),
        "offs": striped(idx),
        "voffs": striped((pages[:, None] * DV + np.arange(DV)[None, :]).reshape(-1)),
    }


def reference(qT, k_words, k_scales, v_words, v_scales, vs, og, offs, voffs):
    idx = unstriped(offs)
    k = unpack_weight(k_words, k_scales, "e4m3")
    v = unpack_weight(v_words, v_scales, "e4m3")
    v = v.reshape(T // 512, 512, DV)[unstriped(voffs)[::DV] // DV].reshape(B, N, DV)
    pick = lambda x: x[:, idx].reshape(x.shape[0], B, N).transpose(1, 0, 2)
    q = f64(qT)
    score = mxq(q, 1, "e4m3").transpose(0, 2, 1) @ pick(k)
    m = score.max(-1, keepdims=True)
    p = np.exp(score - m)
    total = p.sum(-1, keepdims=True)
    w = p * pick(f64(vs))[:, :1, :]
    y = mxq(w, 2, "e4m3") @ v
    y = y / total
    y = y / (1.0 + np.exp(-f64(og)))
    return y

@@ -1,0 +1,221 @@
+from contextlib import ExitStack
+
+import concourse.mybir as mybir
+from concourse.masks import make_identity
+
+B, N, T, D, DV, NQ = 2, 1024, 4096, 512, 256, 128
+P = 128
+PACK = 4
+PAGE = P * PACK
+SEQ_PAGES = N // PAGE
+PAGES = B * SEQ_PAGES
+POOL_PAGES = T // PAGE
+GROUP = 16
+VS_ROW = P - 1
+V_SCALE_ROW = 4
+
+FLOPS = 2 * B * NQ * N * (D + DV)
+
+F32 = mybir.dt.float32
+BF16 = mybir.dt.bfloat16
+I32 = mybir.dt.int32
+U32 = mybir.dt.uint32
+U16 = mybir.dt.uint16
+U8 = mybir.dt.uint8
+FP8X4 = mybir.dt.float8_e4m3fn_x4
+ALU = mybir.AluOpType
+ACT = mybir.ActivationFunctionType
+
+
+def tile_attend_pkv8_gate_kernel(tc, qT, k_words, k_scales, v_words, v_scales, vs, og, offs, voffs, out):
+    nc = tc.nc
+    with ExitStack() as ctx:
+        held = ctx.enter_context(tc.tile_pool(name="held", bufs=1))
+        acc = ctx.enter_context(tc.psum_pool(name="acc", bufs=4))
+        turn = ctx.enter_context(tc.psum_pool(name="turn", bufs=4))
+
+        def entries(lst, first, count):
+            return lst[:, first // GROUP : (first + count) // GROUP]
+
+        slot_list = held.tile([P, B * N // GROUP], U16, name="slot_list")
+        nc.sync.dma_start(slot_list[:], offs)
+
+        k_scale_pool = held.tile([P, T // 4], I32, name="k_scale_pool")
+        nc.vector.memset(k_scale_pool[:], 0)
+        vs_pool = held.tile([P, T], F32, name="vs_pool")
+        nc.sync.dma_start(vs_pool[VS_ROW : VS_ROW + 1, :], vs[0:1, :])
+        nc.vector.memset(vs_pool[0:VS_ROW, :], 0.0)
+
+        q_raw = held.tile([P, B, PACK, NQ], F32, name="q_raw")
+        nc.scalar.dma_start(q_raw[:].rearrange("p b j w -> p b (j w)"), qT.rearrange("b (p j) w -> p b (j w)", j=PACK))
+        k_word_pool = held.tile([P, T], I32, name="k_word_pool")
+        nc.scalar.dma_start(k_word_pool[:], k_words[0].rearrange("p n t -> p (n t)").bitcast(I32))
+        k_scale_rows = k_scales[0].bitcast(I32)
+        for j in range(4):
+            nc.sync.dma_start(k_scale_pool[j:P:32, :], k_scale_rows[j:16:4, :])
+
+        column_list = held.tile([P, B * SEQ_PAGES * DV // GROUP], U16, name="column_list")
+        nc.sync.dma_start(column_list[:], voffs)
+        v_word_pool = held.tile([P, POOL_PAGES * DV], I32, name="v_word_pool")
+        nc.scalar.dma_start(
+            v_word_pool[:].rearrange("p (u e) -> p u e", u=POOL_PAGES),
+            v_words.rearrange("u p e t -> p u (e t)").bitcast(I32),
+        )
+        og_sb = held.tile([P, B, DV], F32, name="og_sb")
+        nc.scalar.dma_start(og_sb[:], og.rearrange("b q e -> q b e"))
+
+        ident = held.tile([P, P], F32, name="ident")
+        make_identity(nc, ident[:])
+
+        vs_slots = held.tile([P, B * N], F32, name="vs_slots")
+        vs_turned = held.tile([P, B * SEQ_PAGES, PACK], F32, name="vs_turned")
+        for b in range(B):
+            nc.vector.tensor_copy(vs_slots[:, b * N : (b + 1) * N], vs_pool[:].indirect(entries(slot_list, b * N, N)))
+        for page in range(B * SEQ_PAGES):
+            bank = turn.tile([P, PACK, P], F32, name="bank")
+            for t in range(PACK):
+                nc.tensor.transpose(bank[:, t, :], vs_slots[:, page * PAGE + t : (page + 1) * PAGE : PACK], ident[:])
+            nc.scalar.copy(vs_turned[:, page, :], bank[:, :, VS_ROW])
+
+        v_scale_pool = held.tile([P, POOL_PAGES * DV // 4], I32, name="v_scale_pool")
+        nc.vector.memset(v_scale_pool[:], 0)
+        v_scale_rows = v_scales.rearrange("u f e -> f u e").bitcast(I32)
+        for j in range(4):
+            nc.sync.dma_start(
+                v_scale_pool[V_SCALE_ROW + j : P : 32, :].rearrange("f (u e) -> f u e", u=POOL_PAGES),
+                v_scale_rows[j:16:4, :, :],
+            )
+
+        k_scale_slots = held.tile([P, B * N], U8, name="k_scale_slots", align_bytes=64)
+        nc.vector.tensor_copy(k_scale_slots[:], k_scale_pool[:].bitcast(U8).indirect(slot_list[:]))
+
+        q_bf = held.tile([P, B, NQ, PACK], BF16, name="q_bf", align_bytes=64)
+        for b in range(B):
+            nc.scalar.activation(q_bf[:, b, :, :], q_raw[:, b, :, :].rearrange("p j w -> p w j"), ACT.Copy)
+        q_codes = held.tile([P, B * NQ], U32, name="q_codes", align_bytes=64)
+        q_scales = held.tile([P, B * NQ], U8, name="q_scales", align_bytes=64)
+        nc.vector.quantize_mx(out=q_codes[:].bitcast(FP8X4), scales=q_scales[:], in_=q_bf[:].rearrange("p b w j -> p (b w j)"))
+
+        k_word_slots = held.tile([P, B * N], U32, name="k_word_slots", align_bytes=64)
+        neg_scores = [held.tile([P, PACK, P], F32, name=f"neg_scores{e}") for e in range(PAGES)]
+        neg_max = [held.tile([P, 1], F32, name=f"neg_max{e}") for e in range(PAGES)]
+        page_sums = [held.tile([P, SEQ_PAGES], F32, name=f"page_sums{b}") for b in range(B)]
+        totals = [held.tile([P, 1], F32, name=f"total{b}") for b in range(B)]
+        scores = []
+        turned = []
+
+        def score(page):
+            b = page // SEQ_PAGES
+            slots = slice(page * PAGE, (page + 1) * PAGE)
+            nc.vector.tensor_copy(k_word_slots[:, slots], k_word_pool[:].bitcast(U32).indirect(entries(slot_list, page * PAGE, PAGE)))
+            bank = acc.tile([P, PAGE], F32, name="score", tag="acc")
+            nc.tensor.matmul_mx(
+                out=bank[:],
+                lhsT=q_codes[:, b * NQ : (b + 1) * NQ].bitcast(FP8X4),
+                lhsT_scale=q_scales[:, b * NQ : (b + 1) * NQ],
+                rhs=k_word_slots[:, slots].bitcast(FP8X4),
+                rhs_scale=k_scale_slots[:, slots],
+                start=True,
+                stop=True,
+            )
+            scores.append(bank)
+
+        def row_max(page):
+            so_far = neg_max[page - 1][:] if page % SEQ_PAGES else None
+            nc.vector.tensor_scalar(
+                neg_scores[page][:],
+                scores[page][:].rearrange("q (s t) -> q t s", t=PACK),
+                -1.0,
+                so_far,
+                ALU.mult,
+                ALU.min,
+                accum_out=neg_max[page][:],
+            )
+
+        def exponentials(b):
+            last = (b + 1) * SEQ_PAGES - 1
+            for h in range(SEQ_PAGES):
+                page = b * SEQ_PAGES + h
+                p_sb = held.tile([P, PACK, P], F32, name=f"p{page}")
+                nc.scalar.activation(
+                    p_sb[:],
+                    neg_scores[page][:],
+                    ACT.Exp,
+                    bias=neg_max[last][:],
+                    scale=-1.0,
+                    accum_out=page_sums[b][:, h : h + 1],
+                )
+                bank = turn.tile([P, PACK, P], F32, name="bank")
+                for t in range(PACK):
+                    nc.tensor.transpose(bank[:, t, :], p_sb[:, t, :], ident[:])
+                turned.append(bank)
+            nc.scalar.activation(totals[b][:], page_sums[b][:, 0:1], ACT.Identity, bias=page_sums[b][:, 1:2], scale=1.0)
+
+        v_word_slots = held.tile([P, PAGES * DV], U32, name="v_word_slots", align_bytes=64)
+        v_scale_slots = held.tile([P, PAGES * DV], U8, name="v_scale_slots", align_bytes=64)
+
+        score(0)
+        score(1)
+        score(2)
+        row_max(0)
+        score(3)
+        row_max(1)
+        exponentials(0)
+        row_max(2)
+        nc.vector.tensor_copy(v_word_slots[:], v_word_pool[:].bitcast(U32).indirect(column_list[:]))
+        row_max(3)
+        exponentials(1)
+        nc.vector.tensor_copy(v_scale_slots[:], v_scale_pool[:].bitcast(U8).indirect(column_list[:]))
+
+        half_tanh = held.tile([P, B * DV], F32, name="half_tanh")
+        nc.scalar.activation(half_tanh[:], og_sb[:].rearrange("q b e -> q (b e)"), ACT.Tanh, scale=0.5)
+        gate = held.tile([P, B * DV], F32, name="gate")
+        nc.scalar.activation(gate[:], half_tanh[:], ACT.Copy, bias=0.5, scale=0.5)
+
+        w_bf = [held.tile([P, NQ, PACK], BF16, name=f"w_bf{e}", align_bytes=64) for e in range(B * SEQ_PAGES)]
+        w_codes = [held.tile([P, NQ], U32, name=f"w_codes{e}", align_bytes=64) for e in range(B * SEQ_PAGES)]
+        w_scales = [held.tile([P, NQ], U8, name=f"w_scales{e}", align_bytes=64) for e in range(B * SEQ_PAGES)]
+        sums = [acc.tile([P, DV], F32, name="sums", tag="acc") for b in range(B)]
+
+        def weigh(page):
+            nc.vector.tensor_tensor(
+                w_bf[page][:],
+                turned[page][:].rearrange("s t q -> s q t"),
+                vs_turned[:, page, :].unsqueeze(1).to_broadcast([P, NQ, PACK]),
+                ALU.mult,
+            )
+
+        def multiply(page):
+            b, h = divmod(page, SEQ_PAGES)
+            nc.vector.quantize_mx(
+                out=w_codes[page][:].bitcast(FP8X4), scales=w_scales[page][:], in_=w_bf[page][:].rearrange("s q t -> s (q t)")
+            )
+            cols = slice(page * DV, (page + 1) * DV)
+            nc.tensor.matmul_mx(
+                out=sums[b][:],
+                lhsT=w_codes[page][:].bitcast(FP8X4),
+                lhsT_scale=w_scales[page][:],
+                rhs=v_word_slots[:, cols].bitcast(FP8X4),
+                rhs_scale=v_scale_slots[V_SCALE_ROW:P, cols],
+                start=(h == 0),
+                stop=(h == SEQ_PAGES - 1),
+            )
+
+        def finish(b):
+            result = held.tile([P, DV], F32, name=f"result{b}")
+            nc.vector.scalar_tensor_tensor(result[:], sums[b][:], inverses[b][:], gate[:, b * DV : (b + 1) * DV], ALU.mult, ALU.mult)
+            nc.sync.dma_start(out[b], result[:])
+
+        inverses = [held.tile([P, 1], F32, name=f"inverse{b}") for b in range(B)]
+        weigh(0)
+        weigh(1)
+        multiply(0)
+        nc.vector.reciprocal(inverses[0][:], totals[0][:])
+        weigh(2)
+        multiply(1)
+        weigh(3)
+        multiply(2)
+        nc.vector.reciprocal(inverses[1][:], totals[1][:])
+        finish(0)
+        multiply(3)
+        finish(1)

@@ -31,54 +31,71 @@ def tile_attend_pkv8_gate_kernel(tc, qT, k_words, k_scales, v_words, v_scales, v
     nc = tc.nc
     with ExitStack() as ctx:
         held = ctx.enter_context(tc.tile_pool(name="held", bufs=1))
+        after_cast = ctx.enter_context(tc.tile_pool(name="after_cast", bufs=1))
+        reused = ctx.enter_context(tc.tile_pool(name="reused", bufs=1))
         acc = ctx.enter_context(tc.psum_pool(name="acc", bufs=4))
         turn = ctx.enter_context(tc.psum_pool(name="turn", bufs=4))
 
-        def entries(lst, first, count):
-            return lst[:, first // GROUP : (first + count) // GROUP]
+        def entries(index_list, first, count):
+            return index_list[:, first // GROUP : (first + count) // GROUP]
 
         slot_list = held.tile([P, B * N // GROUP], U16, name="slot_list")
         nc.sync.dma_start(slot_list[:], offs)
+        vs_pool = held.tile([P, T], F32, name="vs_pool")
+        nc.sync.dma_start(vs_pool[VS_ROW : VS_ROW + 1, :], vs[0:1, :])
+        column_list = held.tile([P, PAGES * DV // GROUP], U16, name="column_list")
+        nc.sync.dma_start(column_list[:], voffs)
+        q_raw = after_cast.tile([P, B, PACK, NQ], F32, name="q_raw", offset=7168)
+        for b in range(B):
+            q_rows = qT[b].rearrange("(p j) w -> p j w", j=PACK)
+            for j in range(0, PACK, 2):
+                nc.sync.dma_start(q_raw[:, b, j : j + 2, :], q_rows[:, j : j + 2, :])
 
         k_scale_pool = held.tile([P, T // 4], I32, name="k_scale_pool")
         nc.vector.memset(k_scale_pool[:], 0)
-        vs_pool = held.tile([P, T], F32, name="vs_pool")
-        nc.sync.dma_start(vs_pool[VS_ROW : VS_ROW + 1, :], vs[0:1, :])
         nc.vector.memset(vs_pool[0:VS_ROW, :], 0.0)
-
-        q_raw = held.tile([P, B, PACK, NQ], F32, name="q_raw")
-        nc.scalar.dma_start(q_raw[:].rearrange("p b j w -> p b (j w)"), qT.rearrange("b (p j) w -> p b (j w)", j=PACK))
-        k_word_pool = held.tile([P, T], I32, name="k_word_pool")
-        nc.scalar.dma_start(k_word_pool[:], k_words[0].rearrange("p n t -> p (n t)").bitcast(I32))
         k_scale_rows = k_scales[0].bitcast(I32)
         for j in range(4):
             nc.sync.dma_start(k_scale_pool[j:P:32, :], k_scale_rows[j:16:4, :])
-
-        column_list = held.tile([P, B * SEQ_PAGES * DV // GROUP], U16, name="column_list")
-        nc.sync.dma_start(column_list[:], voffs)
-        v_word_pool = held.tile([P, POOL_PAGES * DV], I32, name="v_word_pool")
-        nc.scalar.dma_start(
-            v_word_pool[:].rearrange("p (u e) -> p u e", u=POOL_PAGES),
-            v_words.rearrange("u p e t -> p u (e t)").bitcast(I32),
-        )
-        og_sb = held.tile([P, B, DV], F32, name="og_sb")
-        nc.scalar.dma_start(og_sb[:], og.rearrange("b q e -> q b e"))
+        k_word_pool = held.tile([P, T], I32, name="k_word_pool")
+        nc.sync.dma_start(k_word_pool[:], k_words[0].rearrange("p n t -> p (n t)").bitcast(I32))
 
         ident = held.tile([P, P], F32, name="ident")
         make_identity(nc, ident[:])
 
         vs_slots = held.tile([P, B * N], F32, name="vs_slots")
-        vs_turned = held.tile([P, B * SEQ_PAGES, PACK], F32, name="vs_turned")
-        for b in range(B):
-            nc.vector.tensor_copy(vs_slots[:, b * N : (b + 1) * N], vs_pool[:].indirect(entries(slot_list, b * N, N)))
-        for page in range(B * SEQ_PAGES):
-            bank = turn.tile([P, PACK, P], F32, name="bank")
-            for t in range(PACK):
-                nc.tensor.transpose(bank[:, t, :], vs_slots[:, page * PAGE + t : (page + 1) * PAGE : PACK], ident[:])
-            nc.scalar.copy(vs_turned[:, page, :], bank[:, :, VS_ROW])
+        vs_turned = held.tile([P, PAGES, 2 * PACK], F32, name="vs_turned")
+        nc.vector.tensor_copy(vs_slots[:], vs_pool[:].indirect(slot_list[:]))
+        for page in range(PAGES):
+            nc.sync.dma_start(
+                vs_turned[:, page, 0:PACK],
+                vs_slots[VS_ROW : VS_ROW + 1, page * PAGE : (page + 1) * PAGE].rearrange("o (s t) -> o s t", t=PACK),
+            )
 
-        v_scale_pool = held.tile([P, POOL_PAGES * DV // 4], I32, name="v_scale_pool")
-        nc.vector.memset(v_scale_pool[:], 0)
+        k_scale_window = k_scale_pool[:].bitcast(U8)
+        k_scale_slots = held.tile([P, B * N], U8, name="k_scale_slots", align_bytes=64)
+        nc.vector.tensor_copy(k_scale_slots[:], k_scale_window.indirect(slot_list[:]))
+
+        q_bf = held.tile([P, B, NQ, PACK], BF16, name="q_bf", align_bytes=64)
+        for b in range(B):
+            nc.scalar.activation(
+                q_bf[:, b, :, :].rearrange("p (c i) j -> p c j i", i=PACK),
+                q_raw[:, b, :, :].rearrange("p j (c i) -> p c j i", i=PACK),
+                ACT.Copy,
+            )
+        q_codes = held.tile([P, B * NQ], U32, name="q_codes", align_bytes=64)
+        q_scales = held.tile([P, B * NQ], U8, name="q_scales", align_bytes=64)
+        nc.vector.quantize_mx(out=q_codes[:].bitcast(FP8X4), scales=q_scales[:], in_=q_bf[:].rearrange("p b w j -> p (b w j)"))
+
+        og_sb = after_cast.tile([P, B, DV], F32, name="og_sb", offset=10240)
+        nc.sync.dma_start(og_sb[:], og.rearrange("b q e -> q b e"))
+        v_word_pool = after_cast.tile([P, POOL_PAGES * DV], I32, name="v_word_pool", offset=0)
+        nc.sync.dma_start(
+            v_word_pool[:].rearrange("p (u e) -> p u e", u=POOL_PAGES),
+            v_words.rearrange("u p e t -> p u (e t)").bitcast(I32),
+        )
+        v_scale_pool = after_cast.tile([P, POOL_PAGES * DV // 4], I32, name="v_scale_pool", offset=8192)
+        nc.gpsimd.memset(v_scale_pool[:], 0)
         v_scale_rows = v_scales.rearrange("u f e -> f u e").bitcast(I32)
         for j in range(4):
             nc.sync.dma_start(
@@ -86,114 +103,95 @@ def tile_attend_pkv8_gate_kernel(tc, qT, k_words, k_scales, v_words, v_scales, v
                 v_scale_rows[j:16:4, :, :],
             )
 
-        k_scale_slots = held.tile([P, B * N], U8, name="k_scale_slots", align_bytes=64)
-        nc.vector.tensor_copy(k_scale_slots[:], k_scale_pool[:].bitcast(U8).indirect(slot_list[:]))
-
-        q_bf = held.tile([P, B, NQ, PACK], BF16, name="q_bf", align_bytes=64)
-        for b in range(B):
-            nc.scalar.activation(q_bf[:, b, :, :], q_raw[:, b, :, :].rearrange("p j w -> p w j"), ACT.Copy)
-        q_codes = held.tile([P, B * NQ], U32, name="q_codes", align_bytes=64)
-        q_scales = held.tile([P, B * NQ], U8, name="q_scales", align_bytes=64)
-        nc.vector.quantize_mx(out=q_codes[:].bitcast(FP8X4), scales=q_scales[:], in_=q_bf[:].rearrange("p b w j -> p (b w j)"))
-
-        k_word_slots = held.tile([P, B * N], U32, name="k_word_slots", align_bytes=64)
-        neg_scores = [held.tile([P, PACK, P], F32, name=f"neg_scores{e}") for e in range(PAGES)]
-        neg_max = [held.tile([P, 1], F32, name=f"neg_max{e}") for e in range(PAGES)]
-        page_sums = [held.tile([P, SEQ_PAGES], F32, name=f"page_sums{b}") for b in range(B)]
-        totals = [held.tile([P, 1], F32, name=f"total{b}") for b in range(B)]
-        scores = []
-        turned = []
-
-        def score(page):
-            b = page // SEQ_PAGES
-            slots = slice(page * PAGE, (page + 1) * PAGE)
-            nc.vector.tensor_copy(k_word_slots[:, slots], k_word_pool[:].bitcast(U32).indirect(entries(slot_list, page * PAGE, PAGE)))
-            bank = acc.tile([P, PAGE], F32, name="score", tag="acc")
-            nc.tensor.matmul_mx(
-                out=bank[:],
-                lhsT=q_codes[:, b * NQ : (b + 1) * NQ].bitcast(FP8X4),
-                lhsT_scale=q_scales[:, b * NQ : (b + 1) * NQ],
-                rhs=k_word_slots[:, slots].bitcast(FP8X4),
-                rhs_scale=k_scale_slots[:, slots],
-                start=True,
-                stop=True,
-            )
-            scores.append(bank)
-
-        def row_max(page):
-            so_far = neg_max[page - 1][:] if page % SEQ_PAGES else None
-            nc.vector.tensor_scalar(
-                neg_scores[page][:],
-                scores[page][:].rearrange("q (s t) -> q t s", t=PACK),
-                -1.0,
-                so_far,
-                ALU.mult,
-                ALU.min,
-                accum_out=neg_max[page][:],
-            )
-
-        def exponentials(b):
-            last = (b + 1) * SEQ_PAGES - 1
-            for h in range(SEQ_PAGES):
-                page = b * SEQ_PAGES + h
-                p_sb = held.tile([P, PACK, P], F32, name=f"p{page}")
-                nc.scalar.activation(
-                    p_sb[:],
-                    neg_scores[page][:],
-                    ACT.Exp,
-                    bias=neg_max[last][:],
-                    scale=-1.0,
-                    accum_out=page_sums[b][:, h : h + 1],
-                )
-                bank = turn.tile([P, PACK, P], F32, name="bank")
-                for t in range(PACK):
-                    nc.tensor.transpose(bank[:, t, :], p_sb[:, t, :], ident[:])
-                turned.append(bank)
-            nc.scalar.activation(totals[b][:], page_sums[b][:, 0:1], ACT.Identity, bias=page_sums[b][:, 1:2], scale=1.0)
-
-        v_word_slots = held.tile([P, PAGES * DV], U32, name="v_word_slots", align_bytes=64)
-        v_scale_slots = held.tile([P, PAGES * DV], U8, name="v_scale_slots", align_bytes=64)
-
-        score(0)
-        score(1)
-        score(2)
-        row_max(0)
-        score(3)
-        row_max(1)
-        exponentials(0)
-        row_max(2)
-        nc.vector.tensor_copy(v_word_slots[:], v_word_pool[:].bitcast(U32).indirect(column_list[:]))
-        row_max(3)
-        exponentials(1)
-        nc.vector.tensor_copy(v_scale_slots[:], v_scale_pool[:].bitcast(U8).indirect(column_list[:]))
-
-        half_tanh = held.tile([P, B * DV], F32, name="half_tanh")
+        half_tanh = after_cast.tile([P, B * DV], F32, name="half_tanh", offset=12288)
         nc.scalar.activation(half_tanh[:], og_sb[:].rearrange("q b e -> q (b e)"), ACT.Tanh, scale=0.5)
         gate = held.tile([P, B * DV], F32, name="gate")
         nc.scalar.activation(gate[:], half_tanh[:], ACT.Copy, bias=0.5, scale=0.5)
 
-        w_bf = [held.tile([P, NQ, PACK], BF16, name=f"w_bf{e}", align_bytes=64) for e in range(B * SEQ_PAGES)]
-        w_codes = [held.tile([P, NQ], U32, name=f"w_codes{e}", align_bytes=64) for e in range(B * SEQ_PAGES)]
-        w_scales = [held.tile([P, NQ], U8, name=f"w_scales{e}", align_bytes=64) for e in range(B * SEQ_PAGES)]
-        sums = [acc.tile([P, DV], F32, name="sums", tag="acc") for b in range(B)]
+        k_word_slots = [held.tile([P, PAGE], U32, name=f"k_word_slots{e}", align_bytes=64) for e in range(PAGES)]
+        neg_scores = [reused.tile([P, PACK, P], F32, name=f"neg_scores{e}", tag=f"page{e}", align_bytes=64) for e in range(PAGES)]
+        first_max = [held.tile([P, 1], F32, name=f"first_max{b}") for b in range(B)]
+        neg_max = [held.tile([P, 1], F32, name=f"neg_max{b}") for b in range(B)]
+        page_sums = [held.tile([P, SEQ_PAGES], F32, name=f"page_sums{b}") for b in range(B)]
+        totals = [held.tile([P, 1], F32, name=f"total{b}") for b in range(B)]
+        w_scales = [held.tile([P, NQ], U8, name=f"w_scales{e}", align_bytes=64) for e in range(PAGES)]
+        p_sb = after_cast.tile([P, PAGES, PACK, P], F32, name="p_sb", offset=12288)
+        scores = {}
+        turned = {}
+        sums = {}
 
-        def weigh(page):
-            nc.vector.tensor_tensor(
-                w_bf[page][:],
-                turned[page][:].rearrange("s t q -> s q t"),
-                vs_turned[:, page, :].unsqueeze(1).to_broadcast([P, NQ, PACK]),
+        def gather_keys(page):
+            nc.vector.tensor_copy(k_word_slots[page][:], k_word_pool[:].bitcast(U32).indirect(entries(slot_list, page * PAGE, PAGE)))
+
+        def score(page):
+            b = page // SEQ_PAGES
+            scores[page] = acc.tile([P, PAGE], F32, name="score", tag="acc")
+            nc.tensor.matmul_mx(
+                out=scores[page][:],
+                lhsT=q_codes[:, b * NQ : (b + 1) * NQ].bitcast(FP8X4),
+                lhsT_scale=q_scales[:, b * NQ : (b + 1) * NQ],
+                rhs=k_word_slots[page][:].bitcast(FP8X4),
+                rhs_scale=k_scale_slots[:, page * PAGE : (page + 1) * PAGE],
+                start=True,
+                stop=True,
+            )
+
+        def row_max(page):
+            b, h = divmod(page, SEQ_PAGES)
+            nc.vector.tensor_scalar(
+                neg_scores[page][:],
+                scores[page][:].rearrange("q (s t) -> q t s", t=PACK),
+                -1.0,
+                first_max[b][:] if h else None,
                 ALU.mult,
+                ALU.min,
+                accum_out=neg_max[b][:] if h else first_max[b][:],
+            )
+
+        def exponentials(b):
+            for h in range(SEQ_PAGES):
+                page = b * SEQ_PAGES + h
+                nc.scalar.activation(
+                    p_sb[:, page, :, :],
+                    neg_scores[page][:],
+                    ACT.Exp,
+                    bias=neg_max[b][:],
+                    scale=-1.0,
+                    accum_out=page_sums[b][:, h : h + 1],
+                )
+                turned[page] = turn.tile([P, PACK, P], F32, name="turned")
+                for t in range(PACK):
+                    nc.tensor.transpose(turned[page][:, t, :], p_sb[:, page, t, :], ident[:])
+            nc.scalar.activation(totals[b][:], page_sums[b][:, 0:1], ACT.Identity, bias=page_sums[b][:, 1:2], scale=1.0)
+
+        def weigh_on_vector(page):
+            nc.vector.tensor_tensor(
+                w_bf[page // SEQ_PAGES][:, page % SEQ_PAGES, :, :],
+                turned[page][:].rearrange("s t q -> s q t"),
+                vs_turned[:, page, 0:PACK].unsqueeze(1).to_broadcast([P, NQ, PACK]),
+                ALU.mult,
+            )
+
+        def weigh_on_scalar(page):
+            planes = reused.tile([P, PACK, NQ], BF16, name=f"planes{page}", tag=f"page{PAGES - 1 - page}", align_bytes=64)
+            for t in range(PACK):
+                nc.scalar.activation(planes[:, t, :], turned[page][:, t, :], ACT.Copy, scale=vs_turned[:, page, t : t + 1])
+            nc.scalar.copy(
+                w_bf[page // SEQ_PAGES][:, page % SEQ_PAGES, :, :].rearrange("s (c i) t -> s c t i", i=PACK),
+                planes[:].rearrange("s t (c i) -> s c t i", i=PACK),
             )
 
         def multiply(page):
             b, h = divmod(page, SEQ_PAGES)
             nc.vector.quantize_mx(
-                out=w_codes[page][:].bitcast(FP8X4), scales=w_scales[page][:], in_=w_bf[page][:].rearrange("s q t -> s (q t)")
+                out=w_codes[b][:, h, :].bitcast(FP8X4), scales=w_scales[page][:], in_=w_bf[b][:, h, :, :].rearrange("s q t -> s (q t)")
             )
+            if h == 0:
+                sums[b] = acc.tile([P, DV], F32, name="sums", tag="acc")
             cols = slice(page * DV, (page + 1) * DV)
             nc.tensor.matmul_mx(
                 out=sums[b][:],
-                lhsT=w_codes[page][:].bitcast(FP8X4),
+                lhsT=w_codes[b][:, h, :].bitcast(FP8X4),
                 lhsT_scale=w_scales[page][:],
                 rhs=v_word_slots[:, cols].bitcast(FP8X4),
                 rhs_scale=v_scale_slots[V_SCALE_ROW:P, cols],
@@ -203,19 +201,41 @@ def tile_attend_pkv8_gate_kernel(tc, qT, k_words, k_scales, v_words, v_scales, v
 
         def finish(b):
             result = held.tile([P, DV], F32, name=f"result{b}")
-            nc.vector.scalar_tensor_tensor(result[:], sums[b][:], inverses[b][:], gate[:, b * DV : (b + 1) * DV], ALU.mult, ALU.mult)
+            nc.vector.scalar_tensor_tensor(result[:], sums[b][:], inverses[:, b : b + 1], gate[:, b * DV : (b + 1) * DV], ALU.mult, ALU.mult)
             nc.sync.dma_start(out[b], result[:])
 
-        inverses = [held.tile([P, 1], F32, name=f"inverse{b}") for b in range(B)]
-        weigh(0)
-        weigh(1)
+        for page in range(PAGES):
+            gather_keys(page)
+            score(page)
+        for b in range(B):
+            for h in range(SEQ_PAGES):
+                row_max(b * SEQ_PAGES + h)
+            exponentials(b)
+
+        v_word_slots = reused.tile([P, PAGES * DV], U32, name="v_word_slots", tag="page0", align_bytes=64)
+        v_scale_slots = reused.tile([P, PAGES * DV], U8, name="v_scale_slots", tag="page1", align_bytes=64)
+        nc.vector.tensor_copy(v_word_slots[:], v_word_pool[:].bitcast(U32).indirect(column_list[:]))
+        nc.vector.tensor_copy(v_scale_slots[:], v_scale_pool[:].bitcast(U8).indirect(column_list[:]))
+
+        w_bf = [
+            held.tile([P, SEQ_PAGES, NQ, PACK], BF16, name="w_bf0", align_bytes=64),
+            after_cast.tile([P, SEQ_PAGES, NQ, PACK], BF16, name="w_bf1", offset=6208, align_bytes=64),
+        ]
+        w_codes = [
+            after_cast.tile([P, SEQ_PAGES, NQ], U32, name="w_codes0", offset=8256, align_bytes=64),
+            held.tile([P, SEQ_PAGES, NQ], U32, name="w_codes1", align_bytes=64),
+        ]
+        inverses = after_cast.tile([P, B], F32, name="inverses", offset=9280)
+
+        weigh_on_scalar(0)
+        weigh_on_scalar(1)
+        weigh_on_vector(2)
+        for b in range(B):
+            nc.vector.reciprocal(inverses[:, b : b + 1], totals[b][:])
+        weigh_on_vector(3)
         multiply(0)
-        nc.vector.reciprocal(inverses[0][:], totals[0][:])
-        weigh(2)
-        multiply(1)
-        weigh(3)
         multiply(2)
-        nc.vector.reciprocal(inverses[1][:], totals[1][:])
-        finish(0)
         multiply(3)
+        multiply(1)
         finish(1)
+        finish(0)

@@ -78,11 +78,7 @@ def tile_attend_pkv8_gate_kernel(tc, qT, k_words, k_scales, v_words, v_scales, v
 
         q_bf = held.tile([P, B, NQ, PACK], BF16, name="q_bf", align_bytes=64)
         for b in range(B):
-            nc.scalar.activation(
-                q_bf[:, b, :, :].rearrange("p (c i) j -> p c j i", i=PACK),
-                q_raw[:, b, :, :].rearrange("p j (c i) -> p c j i", i=PACK),
-                ACT.Copy,
-            )
+            nc.scalar.activation(q_bf[:, b, :, :], q_raw[:, b, :, :].rearrange("p j w -> p w j"), ACT.Copy)
         q_codes = held.tile([P, B * NQ], U32, name="q_codes", align_bytes=64)
         q_scales = held.tile([P, B * NQ], U8, name="q_scales", align_bytes=64)
         nc.vector.quantize_mx(out=q_codes[:].bitcast(FP8X4), scales=q_scales[:], in_=q_bf[:].rearrange("p b w j -> p (b w j)"))
@@ -108,14 +104,13 @@ def tile_attend_pkv8_gate_kernel(tc, qT, k_words, k_scales, v_words, v_scales, v
         gate = held.tile([P, B * DV], F32, name="gate")
         nc.scalar.activation(gate[:], half_tanh[:], ACT.Copy, bias=0.5, scale=0.5)
 
-        k_word_slots = [held.tile([P, PAGE], U32, name=f"k_word_slots{e}", align_bytes=64) for e in range(PAGES)]
-        neg_scores = [reused.tile([P, PACK, P], F32, name=f"neg_scores{e}", tag=f"page{e}", align_bytes=64) for e in range(PAGES)]
+        k_word_slots = [reused.tile([P, PAGE], U32, name=f"k_word_slots{e}", tag=f"page{e}", align_bytes=64) for e in range(PAGES)]
+        neg_scores = [held.tile([P, PACK, P], F32, name=f"neg_scores{e}") for e in range(PAGES)]
         first_max = [held.tile([P, 1], F32, name=f"first_max{b}") for b in range(B)]
         neg_max = [held.tile([P, 1], F32, name=f"neg_max{b}") for b in range(B)]
         page_sums = [held.tile([P, SEQ_PAGES], F32, name=f"page_sums{b}") for b in range(B)]
-        totals = [held.tile([P, 1], F32, name=f"total{b}") for b in range(B)]
-        w_scales = [held.tile([P, NQ], U8, name=f"w_scales{e}", align_bytes=64) for e in range(PAGES)]
-        p_sb = after_cast.tile([P, PAGES, PACK, P], F32, name="p_sb", offset=12288)
+        totals = held.tile([P, B], F32, name="totals")
+        p_sb = after_cast.tile([P, PAGES, PACK, P], F32, name="p_sb", offset=10240)
         scores = {}
         turned = {}
         sums = {}
@@ -162,42 +157,38 @@ def tile_attend_pkv8_gate_kernel(tc, qT, k_words, k_scales, v_words, v_scales, v
                 turned[page] = turn.tile([P, PACK, P], F32, name="turned")
                 for t in range(PACK):
                     nc.tensor.transpose(turned[page][:, t, :], p_sb[:, page, t, :], ident[:])
-            nc.scalar.activation(totals[b][:], page_sums[b][:, 0:1], ACT.Identity, bias=page_sums[b][:, 1:2], scale=1.0)
+            nc.scalar.activation(totals[:, b : b + 1], page_sums[b][:, 0:1], ACT.Identity, bias=page_sums[b][:, 1:2], scale=1.0)
 
-        def weigh_on_vector(page):
+        def weigh(page):
             nc.vector.tensor_tensor(
-                w_bf[page // SEQ_PAGES][:, page % SEQ_PAGES, :, :],
+                w_bf[:, page, :, :],
                 turned[page][:].rearrange("s t q -> s q t"),
                 vs_turned[:, page, 0:PACK].unsqueeze(1).to_broadcast([P, NQ, PACK]),
                 ALU.mult,
             )
 
-        def weigh_on_scalar(page):
-            planes = reused.tile([P, PACK, NQ], BF16, name=f"planes{page}", tag=f"page{PAGES - 1 - page}", align_bytes=64)
-            for t in range(PACK):
-                nc.scalar.activation(planes[:, t, :], turned[page][:, t, :], ACT.Copy, scale=vs_turned[:, page, t : t + 1])
-            nc.scalar.copy(
-                w_bf[page // SEQ_PAGES][:, page % SEQ_PAGES, :, :].rearrange("s (c i) t -> s c t i", i=PACK),
-                planes[:].rearrange("s t (c i) -> s c t i", i=PACK),
-            )
-
-        def multiply(page):
-            b, h = divmod(page, SEQ_PAGES)
+        def quantise(first, count):
+            cols = slice(first * NQ, (first + count) * NQ)
             nc.vector.quantize_mx(
-                out=w_codes[b][:, h, :].bitcast(FP8X4), scales=w_scales[page][:], in_=w_bf[b][:, h, :, :].rearrange("s q t -> s (q t)")
+                out=w_codes[:, cols].bitcast(FP8X4),
+                scales=w_scales[:, cols],
+                in_=w_bf[:, first : first + count, :, :].rearrange("s h q t -> s (h q t)"),
             )
-            if h == 0:
-                sums[b] = acc.tile([P, DV], F32, name="sums", tag="acc")
-            cols = slice(page * DV, (page + 1) * DV)
-            nc.tensor.matmul_mx(
-                out=sums[b][:],
-                lhsT=w_codes[b][:, h, :].bitcast(FP8X4),
-                lhsT_scale=w_scales[page][:],
-                rhs=v_word_slots[:, cols].bitcast(FP8X4),
-                rhs_scale=v_scale_slots[V_SCALE_ROW:P, cols],
-                start=(h == 0),
-                stop=(h == SEQ_PAGES - 1),
-            )
+            for page in range(first, first + count):
+                b, h = divmod(page, SEQ_PAGES)
+                if h == 0:
+                    sums[b] = acc.tile([P, DV], F32, name="sums", tag="acc")
+                rows = slice(page * NQ, (page + 1) * NQ)
+                cols = slice(page * DV, (page + 1) * DV)
+                nc.tensor.matmul_mx(
+                    out=sums[b][:],
+                    lhsT=w_codes[:, rows].bitcast(FP8X4),
+                    lhsT_scale=w_scales[:, rows],
+                    rhs=v_word_slots[:, cols].bitcast(FP8X4),
+                    rhs_scale=v_scale_slots[V_SCALE_ROW:P, cols],
+                    start=(h == 0),
+                    stop=(h == SEQ_PAGES - 1),
+                )
 
         def finish(b):
             result = held.tile([P, DV], F32, name=f"result{b}")
@@ -207,35 +198,29 @@ def tile_attend_pkv8_gate_kernel(tc, qT, k_words, k_scales, v_words, v_scales, v
         for page in range(PAGES):
             gather_keys(page)
             score(page)
-        for b in range(B):
-            for h in range(SEQ_PAGES):
+        for h in range(SEQ_PAGES):
+            for b in range(B):
                 row_max(b * SEQ_PAGES + h)
+        for b in range(B):
             exponentials(b)
 
-        v_word_slots = reused.tile([P, PAGES * DV], U32, name="v_word_slots", tag="page0", align_bytes=64)
-        v_scale_slots = reused.tile([P, PAGES * DV], U8, name="v_scale_slots", tag="page1", align_bytes=64)
+        v_word_slots = reused.tile([P, PAGES * DV], U32, name="v_word_slots", tag=f"page{PAGES - 1}", align_bytes=64)
+        v_scale_slots = reused.tile([P, PAGES * DV], U8, name="v_scale_slots", tag=f"page{PAGES - 2}", align_bytes=64)
         nc.vector.tensor_copy(v_word_slots[:], v_word_pool[:].bitcast(U32).indirect(column_list[:]))
         nc.vector.tensor_copy(v_scale_slots[:], v_scale_pool[:].bitcast(U8).indirect(column_list[:]))
 
-        w_bf = [
-            held.tile([P, SEQ_PAGES, NQ, PACK], BF16, name="w_bf0", align_bytes=64),
-            after_cast.tile([P, SEQ_PAGES, NQ, PACK], BF16, name="w_bf1", offset=6208, align_bytes=64),
-        ]
-        w_codes = [
-            after_cast.tile([P, SEQ_PAGES, NQ], U32, name="w_codes0", offset=8256, align_bytes=64),
-            held.tile([P, SEQ_PAGES, NQ], U32, name="w_codes1", align_bytes=64),
-        ]
-        inverses = after_cast.tile([P, B], F32, name="inverses", offset=9280)
+        inverses = held.tile([P, B], F32, name="inverses")
+        nc.vector.reciprocal(inverses[:], totals[:])
+        w_bf = after_cast.tile([P, PAGES, NQ, PACK], BF16, name="w_bf", offset=7168, align_bytes=64)
+        w_codes = held.tile([P, PAGES * NQ], U32, name="w_codes", align_bytes=64)
+        w_scales = held.tile([P, PAGES * NQ], U8, name="w_scales", align_bytes=64)
 
-        weigh_on_scalar(0)
-        weigh_on_scalar(1)
-        weigh_on_vector(2)
-        for b in range(B):
-            nc.vector.reciprocal(inverses[:, b : b + 1], totals[b][:])
-        weigh_on_vector(3)
-        multiply(0)
-        multiply(2)
-        multiply(3)
-        multiply(1)
-        finish(1)
+        weigh(0)
+        weigh(1)
+        weigh(2)
+        quantise(0, 2)
+        weigh(3)
+        quantise(2, 1)
+        quantise(3, 1)
         finish(0)
+        finish(1)

@@ -105,12 +105,14 @@ def tile_attend_pkv8_gate_kernel(tc, qT, k_words, k_scales, v_words, v_scales, v
         nc.scalar.activation(gate[:], half_tanh[:], ACT.Copy, bias=0.5, scale=0.5)
 
         k_word_slots = [reused.tile([P, PAGE], U32, name=f"k_word_slots{e}", tag=f"page{e}", align_bytes=64) for e in range(PAGES)]
-        neg_scores = [held.tile([P, PACK, P], F32, name=f"neg_scores{e}") for e in range(PAGES)]
+        neg_scores = [reused.tile([P, PAGE], F32, name=f"neg_scores{e}", tag=f"scores{e}", align_bytes=64) for e in range(PAGES)]
         first_max = [held.tile([P, 1], F32, name=f"first_max{b}") for b in range(B)]
         neg_max = [held.tile([P, 1], F32, name=f"neg_max{b}") for b in range(B)]
         page_sums = [held.tile([P, SEQ_PAGES], F32, name=f"page_sums{b}") for b in range(B)]
         totals = held.tile([P, B], F32, name="totals")
-        p_sb = after_cast.tile([P, PAGES, PACK, P], F32, name="p_sb", offset=10240)
+        p_sb = after_cast.tile([P, PAGES, PACK, P], F32, name="p_sb", offset=12288)
+        w_scales = [held.tile([P, NQ], U8, name=f"w_scales{e}", align_bytes=64) for e in range(PAGES)]
+        planes = {}
         scores = {}
         turned = {}
         sums = {}
@@ -135,7 +137,7 @@ def tile_attend_pkv8_gate_kernel(tc, qT, k_words, k_scales, v_words, v_scales, v
             b, h = divmod(page, SEQ_PAGES)
             nc.vector.tensor_scalar(
                 neg_scores[page][:],
-                scores[page][:].rearrange("q (s t) -> q t s", t=PACK),
+                scores[page][:],
                 -1.0,
                 first_max[b][:] if h else None,
                 ALU.mult,
@@ -147,48 +149,52 @@ def tile_attend_pkv8_gate_kernel(tc, qT, k_words, k_scales, v_words, v_scales, v
             for h in range(SEQ_PAGES):
                 page = b * SEQ_PAGES + h
                 nc.scalar.activation(
-                    p_sb[:, page, :, :],
-                    neg_scores[page][:],
+                    p_sb[:, page, :, :].rearrange("q t s -> q s t"),
+                    neg_scores[page][:].rearrange("q (s t) -> q s t", t=PACK),
                     ACT.Exp,
                     bias=neg_max[b][:],
                     scale=-1.0,
                     accum_out=page_sums[b][:, h : h + 1],
                 )
-                turned[page] = turn.tile([P, PACK, P], F32, name="turned")
+                turned[page] = turn.tile([P, PACK * P], F32, name="turned")
                 for t in range(PACK):
-                    nc.tensor.transpose(turned[page][:, t, :], p_sb[:, page, t, :], ident[:])
+                    place = turned[page][:, t :: PACK] if b else turned[page][:, t * P : (t + 1) * P]
+                    nc.tensor.transpose(place, p_sb[:, page, t, :], ident[:])
             nc.scalar.activation(totals[:, b : b + 1], page_sums[b][:, 0:1], ACT.Identity, bias=page_sums[b][:, 1:2], scale=1.0)
 
-        def weigh(page):
+        def weigh_on_vector(page):
             nc.vector.tensor_tensor(
-                w_bf[:, page, :, :],
-                turned[page][:].rearrange("s t q -> s q t"),
+                w_bf[page // SEQ_PAGES][:, page % SEQ_PAGES, :, :],
+                turned[page][:].rearrange("s (q t) -> s q t", t=PACK),
                 vs_turned[:, page, 0:PACK].unsqueeze(1).to_broadcast([P, NQ, PACK]),
                 ALU.mult,
             )
 
-        def quantise(first, count):
-            cols = slice(first * NQ, (first + count) * NQ)
+        def scale_on_scalar(page):
+            planes[page] = reused.tile([P, PACK, NQ], BF16, name=f"planes{page}", tag=f"scores{PAGES - 1 - page}", align_bytes=64)
+            for t in range(PACK):
+                nc.scalar.activation(planes[page][:, t, :], turned[page][:, t * P : (t + 1) * P], ACT.Copy, scale=vs_turned[:, page, t : t + 1])
+
+        def interleave_on_scalar(page):
+            nc.scalar.copy(w_bf[page // SEQ_PAGES][:, page % SEQ_PAGES, :, :], planes[page][:].rearrange("s t q -> s q t"))
+
+        def multiply(page):
+            b, h = divmod(page, SEQ_PAGES)
             nc.vector.quantize_mx(
-                out=w_codes[:, cols].bitcast(FP8X4),
-                scales=w_scales[:, cols],
-                in_=w_bf[:, first : first + count, :, :].rearrange("s h q t -> s (h q t)"),
+                out=w_codes[b][:, h, :].bitcast(FP8X4), scales=w_scales[page][:], in_=w_bf[b][:, h, :, :].rearrange("s q t -> s (q t)")
             )
-            for page in range(first, first + count):
-                b, h = divmod(page, SEQ_PAGES)
-                if h == 0:
-                    sums[b] = acc.tile([P, DV], F32, name="sums", tag="acc")
-                rows = slice(page * NQ, (page + 1) * NQ)
-                cols = slice(page * DV, (page + 1) * DV)
-                nc.tensor.matmul_mx(
-                    out=sums[b][:],
-                    lhsT=w_codes[:, rows].bitcast(FP8X4),
-                    lhsT_scale=w_scales[:, rows],
-                    rhs=v_word_slots[:, cols].bitcast(FP8X4),
-                    rhs_scale=v_scale_slots[V_SCALE_ROW:P, cols],
-                    start=(h == 0),
-                    stop=(h == SEQ_PAGES - 1),
-                )
+            if h == 0:
+                sums[b] = acc.tile([P, DV], F32, name="sums", tag="acc")
+            cols = slice(page * DV, (page + 1) * DV)
+            nc.tensor.matmul_mx(
+                out=sums[b][:],
+                lhsT=w_codes[b][:, h, :].bitcast(FP8X4),
+                lhsT_scale=w_scales[page][:],
+                rhs=v_word_slots[:, cols].bitcast(FP8X4),
+                rhs_scale=v_scale_slots[V_SCALE_ROW:P, cols],
+                start=(h == 0),
+                stop=(h == SEQ_PAGES - 1),
+            )
 
         def finish(b):
             result = held.tile([P, DV], F32, name=f"result{b}")
@@ -209,18 +215,26 @@ def tile_attend_pkv8_gate_kernel(tc, qT, k_words, k_scales, v_words, v_scales, v
         nc.vector.tensor_copy(v_word_slots[:], v_word_pool[:].bitcast(U32).indirect(column_list[:]))
         nc.vector.tensor_copy(v_scale_slots[:], v_scale_pool[:].bitcast(U8).indirect(column_list[:]))
 
-        inverses = held.tile([P, B], F32, name="inverses")
-        nc.vector.reciprocal(inverses[:], totals[:])
-        w_bf = after_cast.tile([P, PAGES, NQ, PACK], BF16, name="w_bf", offset=7168, align_bytes=64)
-        w_codes = held.tile([P, PAGES * NQ], U32, name="w_codes", align_bytes=64)
-        w_scales = held.tile([P, PAGES * NQ], U8, name="w_scales", align_bytes=64)
+        w_bf = [
+            held.tile([P, SEQ_PAGES, NQ, PACK], BF16, name="w_bf0", align_bytes=64),
+            after_cast.tile([P, SEQ_PAGES, NQ, PACK], BF16, name="w_bf1", offset=6208, align_bytes=64),
+        ]
+        w_codes = [
+            after_cast.tile([P, SEQ_PAGES, NQ], U32, name="w_codes0", offset=8256, align_bytes=64),
+            held.tile([P, SEQ_PAGES, NQ], U32, name="w_codes1", align_bytes=64),
+        ]
+        inverses = after_cast.tile([P, B], F32, name="inverses", offset=9280)
 
-        weigh(0)
-        weigh(1)
-        weigh(2)
-        quantise(0, 2)
-        weigh(3)
-        quantise(2, 1)
-        quantise(3, 1)
-        finish(0)
+        for page in range(SEQ_PAGES):
+            scale_on_scalar(page)
+        for page in range(SEQ_PAGES):
+            interleave_on_scalar(page)
+        weigh_on_vector(2)
+        nc.vector.reciprocal(inverses[:], totals[:])
+        weigh_on_vector(3)
+        multiply(2)
+        multiply(0)
+        multiply(3)
+        multiply(1)
         finish(1)
+        finish(0)

@@ -43,13 +43,9 @@ def tile_attend_pkv8_gate_kernel(tc, qT, k_words, k_scales, v_words, v_scales, v
         nc.sync.dma_start(slot_list[:], offs)
         vs_pool = held.tile([P, T], F32, name="vs_pool")
         nc.sync.dma_start(vs_pool[VS_ROW : VS_ROW + 1, :], vs[0:1, :])
-        column_list = held.tile([P, PAGES * DV // GROUP], U16, name="column_list")
-        nc.sync.dma_start(column_list[:], voffs)
         q_raw = after_cast.tile([P, B, PACK, NQ], F32, name="q_raw", offset=7168)
         for b in range(B):
-            q_rows = qT[b].rearrange("(p j) w -> p j w", j=PACK)
-            for j in range(0, PACK, 2):
-                nc.sync.dma_start(q_raw[:, b, j : j + 2, :], q_rows[:, j : j + 2, :])
+            nc.sync.dma_start(q_raw[:, b, :, :], qT[b].rearrange("(p j) w -> p j w", j=PACK))
 
         k_scale_pool = held.tile([P, T // 4], I32, name="k_scale_pool")
         nc.vector.memset(k_scale_pool[:], 0)
@@ -59,6 +55,10 @@ def tile_attend_pkv8_gate_kernel(tc, qT, k_words, k_scales, v_words, v_scales, v
             nc.sync.dma_start(k_scale_pool[j:P:32, :], k_scale_rows[j:16:4, :])
         k_word_pool = held.tile([P, T], I32, name="k_word_pool")
         nc.sync.dma_start(k_word_pool[:], k_words[0].rearrange("p n t -> p (n t)").bitcast(I32))
+        og_sb = held.tile([P, B, DV], F32, name="og_sb")
+        nc.sync.dma_start(og_sb[:], og.rearrange("b q e -> q b e"))
+        column_list = held.tile([P, PAGES * DV // GROUP], U16, name="column_list")
+        nc.sync.dma_start(column_list[:], voffs)
 
         ident = held.tile([P, P], F32, name="ident")
         make_identity(nc, ident[:])
@@ -83,8 +83,6 @@ def tile_attend_pkv8_gate_kernel(tc, qT, k_words, k_scales, v_words, v_scales, v
         q_scales = held.tile([P, B * NQ], U8, name="q_scales", align_bytes=64)
         nc.vector.quantize_mx(out=q_codes[:].bitcast(FP8X4), scales=q_scales[:], in_=q_bf[:].rearrange("p b w j -> p (b w j)"))
 
-        og_sb = after_cast.tile([P, B, DV], F32, name="og_sb", offset=10240)
-        nc.sync.dma_start(og_sb[:], og.rearrange("b q e -> q b e"))
         v_word_pool = after_cast.tile([P, POOL_PAGES * DV], I32, name="v_word_pool", offset=0)
         nc.sync.dma_start(
             v_word_pool[:].rearrange("p (u e) -> p u e", u=POOL_PAGES),

@@ -59,16 +59,21 @@ def tile_attend_pkv8_gate_kernel(tc, qT, k_words, k_scales, v_words, v_scales, v
         nc.sync.dma_start(og_sb[:], og.rearrange("b q e -> q b e"))
         column_list = held.tile([P, PAGES * DV // GROUP], U16, name="column_list")
         nc.sync.dma_start(column_list[:], voffs)
+        v_word_pool = held.tile([P, POOL_PAGES * DV], I32, name="v_word_pool")
+        nc.sync.dma_start(
+            v_word_pool[:].rearrange("p (u e) -> p u e", u=POOL_PAGES),
+            v_words.rearrange("u p e t -> p u (e t)").bitcast(I32),
+        )
 
         ident = held.tile([P, P], F32, name="ident")
         make_identity(nc, ident[:])
 
         vs_slots = held.tile([P, B * N], F32, name="vs_slots")
-        vs_turned = held.tile([P, PAGES, 2 * PACK], F32, name="vs_turned")
+        vs_turned = [reused.tile([P, SEQ_PAGES, 2 * PACK], F32, name=f"vs_turned{b}", tag=f"vs{b}", align_bytes=64) for b in range(B)]
         nc.vector.tensor_copy(vs_slots[:], vs_pool[:].indirect(slot_list[:]))
         for page in range(PAGES):
             nc.sync.dma_start(
-                vs_turned[:, page, 0:PACK],
+                vs_turned[page // SEQ_PAGES][:, page % SEQ_PAGES, 0:PACK],
                 vs_slots[VS_ROW : VS_ROW + 1, page * PAGE : (page + 1) * PAGE].rearrange("o (s t) -> o s t", t=PACK),
             )
 
@@ -83,16 +88,11 @@ def tile_attend_pkv8_gate_kernel(tc, qT, k_words, k_scales, v_words, v_scales, v
         q_scales = held.tile([P, B * NQ], U8, name="q_scales", align_bytes=64)
         nc.vector.quantize_mx(out=q_codes[:].bitcast(FP8X4), scales=q_scales[:], in_=q_bf[:].rearrange("p b w j -> p (b w j)"))
 
-        v_word_pool = after_cast.tile([P, POOL_PAGES * DV], I32, name="v_word_pool", offset=0)
-        nc.sync.dma_start(
-            v_word_pool[:].rearrange("p (u e) -> p u e", u=POOL_PAGES),
-            v_words.rearrange("u p e t -> p u (e t)").bitcast(I32),
-        )
         v_scale_pool = after_cast.tile([P, POOL_PAGES * DV // 4], I32, name="v_scale_pool", offset=8192)
         nc.gpsimd.memset(v_scale_pool[:], 0)
         v_scale_rows = v_scales.rearrange("u f e -> f u e").bitcast(I32)
         for j in range(4):
-            nc.sync.dma_start(
+            nc.scalar.dma_start(
                 v_scale_pool[V_SCALE_ROW + j : P : 32, :].rearrange("f (u e) -> f u e", u=POOL_PAGES),
                 v_scale_rows[j:16:4, :, :],
             )
@@ -108,7 +108,7 @@ def tile_attend_pkv8_gate_kernel(tc, qT, k_words, k_scales, v_words, v_scales, v
         neg_max = [held.tile([P, 1], F32, name=f"neg_max{b}") for b in range(B)]
         page_sums = [held.tile([P, SEQ_PAGES], F32, name=f"page_sums{b}") for b in range(B)]
         totals = held.tile([P, B], F32, name="totals")
-        p_sb = after_cast.tile([P, PAGES, PACK, P], F32, name="p_sb", offset=12288)
+        p_sb = [after_cast.tile([P, SEQ_PAGES, PACK, P], F32, name=f"p_sb{b}", offset=12288 + 4096 * b) for b in range(B)]
         w_scales = [held.tile([P, NQ], U8, name=f"w_scales{e}", align_bytes=64) for e in range(PAGES)]
         planes = {}
         scores = {}
@@ -147,7 +147,7 @@ def tile_attend_pkv8_gate_kernel(tc, qT, k_words, k_scales, v_words, v_scales, v
             for h in range(SEQ_PAGES):
                 page = b * SEQ_PAGES + h
                 nc.scalar.activation(
-                    p_sb[:, page, :, :].rearrange("q t s -> q s t"),
+                    p_sb[b][:, h, :, :].rearrange("q t s -> q s t"),
                     neg_scores[page][:].rearrange("q (s t) -> q s t", t=PACK),
                     ACT.Exp,
                     bias=neg_max[b][:],
@@ -156,22 +156,21 @@ def tile_attend_pkv8_gate_kernel(tc, qT, k_words, k_scales, v_words, v_scales, v
                 )
                 turned[page] = turn.tile([P, PACK * P], F32, name="turned")
                 for t in range(PACK):
-                    place = turned[page][:, t :: PACK] if b else turned[page][:, t * P : (t + 1) * P]
-                    nc.tensor.transpose(place, p_sb[:, page, t, :], ident[:])
-            nc.scalar.activation(totals[:, b : b + 1], page_sums[b][:, 0:1], ACT.Identity, bias=page_sums[b][:, 1:2], scale=1.0)
+                    place = turned[page][:, t * P : (t + 1) * P] if b else turned[page][:, t :: PACK]
+                    nc.tensor.transpose(place, p_sb[b][:, h, t, :], ident[:])
 
         def weigh_on_vector(page):
             nc.vector.tensor_tensor(
                 w_bf[page // SEQ_PAGES][:, page % SEQ_PAGES, :, :],
                 turned[page][:].rearrange("s (q t) -> s q t", t=PACK),
-                vs_turned[:, page, 0:PACK].unsqueeze(1).to_broadcast([P, NQ, PACK]),
+                vs_turned[0][:, page, 0:PACK].unsqueeze(1).to_broadcast([P, NQ, PACK]),
                 ALU.mult,
             )
 
         def scale_on_scalar(page):
-            planes[page] = reused.tile([P, PACK, NQ], BF16, name=f"planes{page}", tag=f"scores{PAGES - 1 - page}", align_bytes=64)
+            planes[page] = reused.tile([P, PACK, NQ], BF16, name=f"planes{page}", tag=f"scores{PAGES + SEQ_PAGES - 1 - page}", align_bytes=64)
             for t in range(PACK):
-                nc.scalar.activation(planes[page][:, t, :], turned[page][:, t * P : (t + 1) * P], ACT.Copy, scale=vs_turned[:, page, t : t + 1])
+                nc.scalar.activation(planes[page][:, t, :], turned[page][:, t * P : (t + 1) * P], ACT.Copy, scale=vs_turned[1][:, page - SEQ_PAGES, t : t + 1])
 
         def interleave_on_scalar(page):
             nc.scalar.copy(w_bf[page // SEQ_PAGES][:, page % SEQ_PAGES, :, :], planes[page][:].rearrange("s t q -> s q t"))
@@ -188,14 +187,14 @@ def tile_attend_pkv8_gate_kernel(tc, qT, k_words, k_scales, v_words, v_scales, v
                 out=sums[b][:],
                 lhsT=w_codes[b][:, h, :].bitcast(FP8X4),
                 lhsT_scale=w_scales[page][:],
-                rhs=v_word_slots[:, cols].bitcast(FP8X4),
+                rhs=v_word_slots[page].bitcast(FP8X4),
                 rhs_scale=v_scale_slots[V_SCALE_ROW:P, cols],
                 start=(h == 0),
                 stop=(h == SEQ_PAGES - 1),
             )
 
         def finish(b):
-            result = held.tile([P, DV], F32, name=f"result{b}")
+            result = reused.tile([P, DV], F32, name=f"result{b}", tag="result" if b else "last", align_bytes=64)
             nc.vector.scalar_tensor_tensor(result[:], sums[b][:], inverses[:, b : b + 1], gate[:, b * DV : (b + 1) * DV], ALU.mult, ALU.mult)
             nc.sync.dma_start(out[b], result[:])
 
@@ -208,31 +207,37 @@ def tile_attend_pkv8_gate_kernel(tc, qT, k_words, k_scales, v_words, v_scales, v
         for b in range(B):
             exponentials(b)
 
-        v_word_slots = reused.tile([P, PAGES * DV], U32, name="v_word_slots", tag=f"page{PAGES - 1}", align_bytes=64)
+        def gather_values(first, count, tag):
+            slots = reused.tile([P, count * DV], U32, name=f"v_word_slots{first}", tag=tag, align_bytes=64)
+            nc.vector.tensor_copy(slots[:], v_word_pool[:].bitcast(U32).indirect(entries(column_list, first * DV, count * DV)))
+            for e in range(count):
+                v_word_slots[first + e] = slots[:, e * DV : (e + 1) * DV]
+
+        v_word_slots = {}
         v_scale_slots = reused.tile([P, PAGES * DV], U8, name="v_scale_slots", tag=f"page{PAGES - 2}", align_bytes=64)
-        nc.vector.tensor_copy(v_word_slots[:], v_word_pool[:].bitcast(U32).indirect(column_list[:]))
         nc.vector.tensor_copy(v_scale_slots[:], v_scale_pool[:].bitcast(U8).indirect(column_list[:]))
+        gather_values(0, PAGES - 1, f"page{PAGES - 1}")
 
         w_bf = [
-            held.tile([P, SEQ_PAGES, NQ, PACK], BF16, name="w_bf0", align_bytes=64),
-            after_cast.tile([P, SEQ_PAGES, NQ, PACK], BF16, name="w_bf1", offset=6208, align_bytes=64),
+            after_cast.tile([P, SEQ_PAGES, NQ, PACK], BF16, name="w_bf0", offset=16384, align_bytes=64),
+            reused.tile([P, SEQ_PAGES, NQ, PACK], BF16, name="w_bf1", tag="last", align_bytes=64),
         ]
-        w_codes = [
-            after_cast.tile([P, SEQ_PAGES, NQ], U32, name="w_codes0", offset=8256, align_bytes=64),
-            held.tile([P, SEQ_PAGES, NQ], U32, name="w_codes1", align_bytes=64),
-        ]
-        inverses = after_cast.tile([P, B], F32, name="inverses", offset=9280)
+        w_codes = [held.tile([P, SEQ_PAGES, NQ], U32, name=f"w_codes{b}", align_bytes=64) for b in range(B)]
+        inverses = held.tile([P, B], F32, name="inverses")
 
-        for page in range(SEQ_PAGES):
+        for page in (2, 3):
             scale_on_scalar(page)
-        for page in range(SEQ_PAGES):
+        for page in (2, 3):
             interleave_on_scalar(page)
-        weigh_on_vector(2)
-        nc.vector.reciprocal(inverses[:], totals[:])
-        weigh_on_vector(3)
-        multiply(2)
+        for b in range(B):
+            nc.scalar.activation(totals[:, b : b + 1], page_sums[b][:, 0:1], ACT.Identity, bias=page_sums[b][:, 1:2], scale=1.0)
+        weigh_on_vector(0)
+        weigh_on_vector(1)
         multiply(0)
-        multiply(3)
         multiply(1)
-        finish(1)
+        multiply(2)
+        gather_values(3, 1, "scores3")
+        multiply(3)
+        nc.vector.reciprocal(inverses[:], totals[:])
         finish(0)
+        finish(1)

@@ -33,6 +33,7 @@ def tile_attend_pkv8_gate_kernel(tc, qT, k_words, k_scales, v_words, v_scales, v
         held = ctx.enter_context(tc.tile_pool(name="held", bufs=1))
         after_cast = ctx.enter_context(tc.tile_pool(name="after_cast", bufs=1))
         reused = ctx.enter_context(tc.tile_pool(name="reused", bufs=1))
+        late = ctx.enter_context(tc.tile_pool(name="late", bufs=1))
         acc = ctx.enter_context(tc.psum_pool(name="acc", bufs=4))
         turn = ctx.enter_context(tc.psum_pool(name="turn", bufs=4))
 
@@ -68,14 +69,18 @@ def tile_attend_pkv8_gate_kernel(tc, qT, k_words, k_scales, v_words, v_scales, v
         ident = held.tile([P, P], F32, name="ident")
         make_identity(nc, ident[:])
 
-        vs_slots = held.tile([P, B * N], F32, name="vs_slots")
-        vs_turned = [reused.tile([P, SEQ_PAGES, 2 * PACK], F32, name=f"vs_turned{b}", tag=f"vs{b}", align_bytes=64) for b in range(B)]
-        nc.vector.tensor_copy(vs_slots[:], vs_pool[:].indirect(slot_list[:]))
-        for page in range(PAGES):
-            nc.sync.dma_start(
-                vs_turned[page // SEQ_PAGES][:, page % SEQ_PAGES, 0:PACK],
-                vs_slots[VS_ROW : VS_ROW + 1, page * PAGE : (page + 1) * PAGE].rearrange("o (s t) -> o s t", t=PACK),
-            )
+        vs_turned = [held.tile([P, SEQ_PAGES, 2 * PACK], F32, name=f"vs_turned{b}") for b in range(B)]
+
+        def gather_vs(slots, first, count):
+            nc.vector.tensor_copy(slots[:], vs_pool[:].indirect(entries(slot_list, first * PAGE, count * PAGE)))
+            for e in range(count):
+                b, h = divmod(first + e, SEQ_PAGES)
+                nc.sync.dma_start(
+                    vs_turned[b][:, h, 0:PACK],
+                    slots[VS_ROW : VS_ROW + 1, e * PAGE : (e + 1) * PAGE].rearrange("o (s t) -> o s t", t=PACK),
+                )
+
+        gather_vs(held.tile([P, (PAGES - 1) * PAGE], F32, name="vs_slots"), 1, PAGES - 1)
 
         k_scale_window = k_scale_pool[:].bitcast(U8)
         k_scale_slots = held.tile([P, B * N], U8, name="k_scale_slots", align_bytes=64)
@@ -102,7 +107,8 @@ def tile_attend_pkv8_gate_kernel(tc, qT, k_words, k_scales, v_words, v_scales, v
         gate = held.tile([P, B * DV], F32, name="gate")
         nc.scalar.activation(gate[:], half_tanh[:], ACT.Copy, bias=0.5, scale=0.5)
 
-        k_word_slots = [reused.tile([P, PAGE], U32, name=f"k_word_slots{e}", tag=f"page{e}", align_bytes=64) for e in range(PAGES)]
+        k_word_slots = [reused.tile([P, PAGE], U32, name=f"k_word_slots{e}", tag=f"page{e}", align_bytes=64) for e in range(PAGES - 1)]
+        k_word_slots.append(late.tile([P, PAGE], U32, name="k_word_slots_last", offset=1024, align_bytes=64))
         neg_scores = [reused.tile([P, PAGE], F32, name=f"neg_scores{e}", tag=f"scores{e}", align_bytes=64) for e in range(PAGES)]
         first_max = [held.tile([P, 1], F32, name=f"first_max{b}") for b in range(B)]
         neg_max = [held.tile([P, 1], F32, name=f"neg_max{b}") for b in range(B)]
@@ -180,7 +186,8 @@ def tile_attend_pkv8_gate_kernel(tc, qT, k_words, k_scales, v_words, v_scales, v
             nc.vector.quantize_mx(
                 out=w_codes[b][:, h, :].bitcast(FP8X4), scales=w_scales[page][:], in_=w_bf[b][:, h, :, :].rearrange("s q t -> s (q t)")
             )
-            if h == 0:
+            first = b not in sums
+            if first:
                 sums[b] = acc.tile([P, DV], F32, name="sums", tag="acc")
             cols = slice(page * DV, (page + 1) * DV)
             nc.tensor.matmul_mx(
@@ -189,8 +196,8 @@ def tile_attend_pkv8_gate_kernel(tc, qT, k_words, k_scales, v_words, v_scales, v
                 lhsT_scale=w_scales[page][:],
                 rhs=v_word_slots[page].bitcast(FP8X4),
                 rhs_scale=v_scale_slots[V_SCALE_ROW:P, cols],
-                start=(h == 0),
-                stop=(h == SEQ_PAGES - 1),
+                start=first,
+                stop=not first,
             )
 
         def finish(b):
@@ -207,16 +214,16 @@ def tile_attend_pkv8_gate_kernel(tc, qT, k_words, k_scales, v_words, v_scales, v
         for b in range(B):
             exponentials(b)
 
-        def gather_values(first, count, tag):
-            slots = reused.tile([P, count * DV], U32, name=f"v_word_slots{first}", tag=tag, align_bytes=64)
+        def gather_values(slots, first, count):
             nc.vector.tensor_copy(slots[:], v_word_pool[:].bitcast(U32).indirect(entries(column_list, first * DV, count * DV)))
             for e in range(count):
                 v_word_slots[first + e] = slots[:, e * DV : (e + 1) * DV]
 
+        gather_vs(late.tile([P, PAGE], F32, name="vs_slots_first", offset=0, align_bytes=64), 0, 1)
         v_word_slots = {}
         v_scale_slots = reused.tile([P, PAGES * DV], U8, name="v_scale_slots", tag=f"page{PAGES - 2}", align_bytes=64)
         nc.vector.tensor_copy(v_scale_slots[:], v_scale_pool[:].bitcast(U8).indirect(column_list[:]))
-        gather_values(0, PAGES - 1, f"page{PAGES - 1}")
+        gather_values(late.tile([P, (PAGES - 1) * DV], U32, name="v_word_slots", offset=2048, align_bytes=64), 0, PAGES - 1)
 
         w_bf = [
             after_cast.tile([P, SEQ_PAGES, NQ, PACK], BF16, name="w_bf0", offset=16384, align_bytes=64),
@@ -231,12 +238,12 @@ def tile_attend_pkv8_gate_kernel(tc, qT, k_words, k_scales, v_words, v_scales, v
             interleave_on_scalar(page)
         for b in range(B):
             nc.scalar.activation(totals[:, b : b + 1], page_sums[b][:, 0:1], ACT.Identity, bias=page_sums[b][:, 1:2], scale=1.0)
-        weigh_on_vector(0)
         weigh_on_vector(1)
-        multiply(0)
+        weigh_on_vector(0)
         multiply(1)
+        multiply(0)
         multiply(2)
-        gather_values(3, 1, "scores3")
+        gather_values(reused.tile([P, DV], U32, name="v_word_slots_last", tag="scores3", align_bytes=64), 3, 1)
         multiply(3)
         nc.vector.reciprocal(inverses[:], totals[:])
         finish(0)

@@ -9,10 +9,21 @@ PACK = 4
 PAGE = P * PACK
 SEQ_PAGES = N // PAGE
 PAGES = B * SEQ_PAGES
+LAST = PAGES - 1
 POOL_PAGES = T // PAGE
 GROUP = 16
+QUADRANT = 32
 VS_ROW = P - 1
 V_SCALE_ROW = 4
+VS_PITCH = 2 * PACK
+
+Q_RAW_BYTES = PACK * NQ * 4
+Q_RAW_AT = (0, Q_RAW_BYTES)
+P_BYTES = SEQ_PAGES * PAGE * 4
+P_AT = (B * Q_RAW_BYTES, B * Q_RAW_BYTES + P_BYTES)
+V_SCALE_SLOTS_AT = 0
+NEG_SCORES1_AT = V_SCALE_SLOTS_AT + PAGES * DV // 2
+V_WORD_SLOTS_AT = V_SCALE_SLOTS_AT + PAGES * DV
 
 FLOPS = 2 * B * NQ * N * (D + DV)
 
@@ -31,11 +42,11 @@ def tile_attend_pkv8_gate_kernel(tc, qT, k_words, k_scales, v_words, v_scales, v
     nc = tc.nc
     with ExitStack() as ctx:
         held = ctx.enter_context(tc.tile_pool(name="held", bufs=1))
-        after_cast = ctx.enter_context(tc.tile_pool(name="after_cast", bufs=1))
+        staged = ctx.enter_context(tc.tile_pool(name="staged", bufs=1))
         reused = ctx.enter_context(tc.tile_pool(name="reused", bufs=1))
         late = ctx.enter_context(tc.tile_pool(name="late", bufs=1))
-        acc = ctx.enter_context(tc.psum_pool(name="acc", bufs=4))
-        turn = ctx.enter_context(tc.psum_pool(name="turn", bufs=4))
+        acc = ctx.enter_context(tc.psum_pool(name="acc", bufs=PAGES))
+        turn = ctx.enter_context(tc.psum_pool(name="turn", bufs=PAGES))
 
         def entries(index_list, first, count):
             return index_list[:, first // GROUP : (first + count) // GROUP]
@@ -44,32 +55,32 @@ def tile_attend_pkv8_gate_kernel(tc, qT, k_words, k_scales, v_words, v_scales, v
         nc.sync.dma_start(slot_list[:], offs)
         vs_pool = held.tile([P, T], F32, name="vs_pool")
         nc.sync.dma_start(vs_pool[VS_ROW : VS_ROW + 1, :], vs[0:1, :])
-        q_raw = after_cast.tile([P, B, PACK, NQ], F32, name="q_raw", offset=7168)
-        for b in range(B):
-            nc.sync.dma_start(q_raw[:, b, :, :], qT[b].rearrange("(p j) w -> p j w", j=PACK))
+        q_raw = [staged.tile([P, PACK, NQ], F32, name=f"q_raw{b}", offset=Q_RAW_AT[b]) for b in range(B)]
+        nc.sync.dma_start(q_raw[0][:], qT[0].rearrange("(g r) q -> g r q", r=PACK))
+        column_list = held.tile([P, PAGES * DV // GROUP], U16, name="column_list")
+        nc.sync.dma_start(column_list[:], voffs)
 
         k_scale_pool = held.tile([P, T // 4], I32, name="k_scale_pool")
         nc.vector.memset(k_scale_pool[:], 0)
         nc.vector.memset(vs_pool[0:VS_ROW, :], 0.0)
         k_scale_rows = k_scales[0].bitcast(I32)
         for j in range(4):
-            nc.sync.dma_start(k_scale_pool[j:P:32, :], k_scale_rows[j:16:4, :])
+            nc.sync.dma_start(k_scale_pool[j:P:QUADRANT, :], k_scale_rows[j:16:4, :])
         k_word_pool = held.tile([P, T], I32, name="k_word_pool")
-        nc.sync.dma_start(k_word_pool[:], k_words[0].rearrange("p n t -> p (n t)").bitcast(I32))
+        nc.sync.dma_start(k_word_pool[:], k_words[0].rearrange("g t r -> g (t r)").bitcast(I32))
+        nc.sync.dma_start(q_raw[1][:], qT[1].rearrange("(g r) q -> g r q", r=PACK))
         og_sb = held.tile([P, B, DV], F32, name="og_sb")
         nc.sync.dma_start(og_sb[:], og.rearrange("b q e -> q b e"))
-        column_list = held.tile([P, PAGES * DV // GROUP], U16, name="column_list")
-        nc.sync.dma_start(column_list[:], voffs)
         v_word_pool = held.tile([P, POOL_PAGES * DV], I32, name="v_word_pool")
         nc.sync.dma_start(
-            v_word_pool[:].rearrange("p (u e) -> p u e", u=POOL_PAGES),
-            v_words.rearrange("u p e t -> p u (e t)").bitcast(I32),
+            v_word_pool[:].rearrange("g (u e) -> g u e", u=POOL_PAGES),
+            v_words.rearrange("u g e r -> g u (e r)").bitcast(I32),
         )
 
         ident = held.tile([P, P], F32, name="ident")
         make_identity(nc, ident[:])
 
-        vs_turned = [held.tile([P, SEQ_PAGES, 2 * PACK], F32, name=f"vs_turned{b}") for b in range(B)]
+        vs_turned = [held.tile([P, SEQ_PAGES, VS_PITCH], F32, name=f"vs_turned{b}") for b in range(B)]
 
         def gather_vs(slots, first, count):
             nc.vector.tensor_copy(slots[:], vs_pool[:].indirect(entries(slot_list, first * PAGE, count * PAGE)))
@@ -77,61 +88,63 @@ def tile_attend_pkv8_gate_kernel(tc, qT, k_words, k_scales, v_words, v_scales, v
                 b, h = divmod(first + e, SEQ_PAGES)
                 nc.sync.dma_start(
                     vs_turned[b][:, h, 0:PACK],
-                    slots[VS_ROW : VS_ROW + 1, e * PAGE : (e + 1) * PAGE].rearrange("o (s t) -> o s t", t=PACK),
+                    slots[VS_ROW : VS_ROW + 1, e * PAGE : (e + 1) * PAGE].rearrange("o (g r) -> o g r", r=PACK),
                 )
 
-        gather_vs(held.tile([P, (PAGES - 1) * PAGE], F32, name="vs_slots"), 1, PAGES - 1)
+        gather_vs(held.tile([P, LAST * PAGE], F32, name="vs_slots"), 1, LAST)
 
-        k_scale_window = k_scale_pool[:].bitcast(U8)
         k_scale_slots = held.tile([P, B * N], U8, name="k_scale_slots", align_bytes=64)
-        nc.vector.tensor_copy(k_scale_slots[:], k_scale_window.indirect(slot_list[:]))
+        nc.vector.tensor_copy(k_scale_slots[:], k_scale_pool[:].bitcast(U8).indirect(slot_list[:]))
 
-        q_bf = held.tile([P, B, NQ, PACK], BF16, name="q_bf", align_bytes=64)
+        q_bf = [held.tile([P, NQ, PACK], BF16, name=f"q_bf{b}", align_bytes=64) for b in range(B)]
+        q_codes = [held.tile([P, NQ], U32, name=f"q_codes{b}", align_bytes=64) for b in range(B)]
+        q_scales = [held.tile([P, NQ], U8, name=f"q_scales{b}", align_bytes=64) for b in range(B)]
         for b in range(B):
-            nc.scalar.activation(q_bf[:, b, :, :], q_raw[:, b, :, :].rearrange("p j w -> p w j"), ACT.Copy)
-        q_codes = held.tile([P, B * NQ], U32, name="q_codes", align_bytes=64)
-        q_scales = held.tile([P, B * NQ], U8, name="q_scales", align_bytes=64)
-        nc.vector.quantize_mx(out=q_codes[:].bitcast(FP8X4), scales=q_scales[:], in_=q_bf[:].rearrange("p b w j -> p (b w j)"))
+            nc.scalar.activation(q_bf[b][:], q_raw[b][:].rearrange("g r q -> g q r"), ACT.Copy)
+            nc.vector.quantize_mx(out=q_codes[b][:].bitcast(FP8X4), scales=q_scales[b][:], in_=q_bf[b][:].rearrange("g q r -> g (q r)"))
 
-        v_scale_pool = after_cast.tile([P, POOL_PAGES * DV // 4], I32, name="v_scale_pool", offset=8192)
+        v_scale_pool = staged.tile([P, POOL_PAGES * DV // 4], I32, name="v_scale_pool", offset=Q_RAW_AT[1])
         nc.gpsimd.memset(v_scale_pool[:], 0)
         v_scale_rows = v_scales.rearrange("u f e -> f u e").bitcast(I32)
         for j in range(4):
             nc.scalar.dma_start(
-                v_scale_pool[V_SCALE_ROW + j : P : 32, :].rearrange("f (u e) -> f u e", u=POOL_PAGES),
+                v_scale_pool[V_SCALE_ROW + j : P : QUADRANT, :].rearrange("f (u e) -> f u e", u=POOL_PAGES),
                 v_scale_rows[j:16:4, :, :],
             )
 
-        half_tanh = after_cast.tile([P, B * DV], F32, name="half_tanh", offset=12288)
+        half_tanh = staged.tile([P, B * DV], F32, name="half_tanh", offset=P_AT[0])
         nc.scalar.activation(half_tanh[:], og_sb[:].rearrange("q b e -> q (b e)"), ACT.Tanh, scale=0.5)
         gate = held.tile([P, B * DV], F32, name="gate")
         nc.scalar.activation(gate[:], half_tanh[:], ACT.Copy, bias=0.5, scale=0.5)
 
-        k_word_slots = [reused.tile([P, PAGE], U32, name=f"k_word_slots{e}", tag=f"page{e}", align_bytes=64) for e in range(PAGES - 1)]
-        k_word_slots.append(late.tile([P, PAGE], U32, name="k_word_slots_last", offset=1024, align_bytes=64))
-        neg_scores = [reused.tile([P, PAGE], F32, name=f"neg_scores{e}", tag=f"scores{e}", align_bytes=64) for e in range(PAGES)]
-        first_max = [held.tile([P, 1], F32, name=f"first_max{b}") for b in range(B)]
+        neg_scores = [
+            late.tile([P, PAGE], F32, name="neg_scores1", offset=NEG_SCORES1_AT, align_bytes=64)
+            if page == SEQ_PAGES - 1
+            else reused.tile([P, PAGE], F32, name=f"neg_scores{page}", tag=f"scores{page}", align_bytes=64)
+            for page in range(PAGES)
+        ]
+        first_neg_max = [held.tile([P, 1], F32, name=f"first_neg_max{b}") for b in range(B)]
         neg_max = [held.tile([P, 1], F32, name=f"neg_max{b}") for b in range(B)]
         page_sums = [held.tile([P, SEQ_PAGES], F32, name=f"page_sums{b}") for b in range(B)]
         totals = held.tile([P, B], F32, name="totals")
-        p_sb = [after_cast.tile([P, SEQ_PAGES, PACK, P], F32, name=f"p_sb{b}", offset=12288 + 4096 * b) for b in range(B)]
-        w_scales = [held.tile([P, NQ], U8, name=f"w_scales{e}", align_bytes=64) for e in range(PAGES)]
-        planes = {}
+        p_sb = [staged.tile([P, SEQ_PAGES, PACK, P], F32, name=f"p_sb{b}", offset=P_AT[b]) for b in range(B)]
+        w_scales = [held.tile([P, NQ], U8, name=f"w_scales{page}", align_bytes=64) for page in range(PAGES)]
         scores = {}
         turned = {}
+        planes = {}
+        v_word_slots = {}
         sums = {}
-
-        def gather_keys(page):
-            nc.vector.tensor_copy(k_word_slots[page][:], k_word_pool[:].bitcast(U32).indirect(entries(slot_list, page * PAGE, PAGE)))
 
         def score(page):
             b = page // SEQ_PAGES
+            keys = reused.tile([P, PAGE], U32, name=f"k_word_slots{page}", tag=f"keys{page % LAST}", align_bytes=64)
+            nc.vector.tensor_copy(keys[:], k_word_pool[:].bitcast(U32).indirect(entries(slot_list, page * PAGE, PAGE)))
             scores[page] = acc.tile([P, PAGE], F32, name="score", tag="acc")
             nc.tensor.matmul_mx(
                 out=scores[page][:],
-                lhsT=q_codes[:, b * NQ : (b + 1) * NQ].bitcast(FP8X4),
-                lhsT_scale=q_scales[:, b * NQ : (b + 1) * NQ],
-                rhs=k_word_slots[page][:].bitcast(FP8X4),
+                lhsT=q_codes[b][:].bitcast(FP8X4),
+                lhsT_scale=q_scales[b][:],
+                rhs=keys[:].bitcast(FP8X4),
                 rhs_scale=k_scale_slots[:, page * PAGE : (page + 1) * PAGE],
                 start=True,
                 stop=True,
@@ -143,108 +156,113 @@ def tile_attend_pkv8_gate_kernel(tc, qT, k_words, k_scales, v_words, v_scales, v
                 neg_scores[page][:],
                 scores[page][:],
                 -1.0,
-                first_max[b][:] if h else None,
+                first_neg_max[b][:] if h else None,
                 ALU.mult,
                 ALU.min,
-                accum_out=neg_max[b][:] if h else first_max[b][:],
+                accum_out=neg_max[b][:] if h else first_neg_max[b][:],
             )
 
         def exponentials(b):
             for h in range(SEQ_PAGES):
                 page = b * SEQ_PAGES + h
                 nc.scalar.activation(
-                    p_sb[b][:, h, :, :].rearrange("q t s -> q s t"),
-                    neg_scores[page][:].rearrange("q (s t) -> q s t", t=PACK),
+                    p_sb[b][:, h, :, :].rearrange("q r g -> q g r"),
+                    neg_scores[page][:].rearrange("q (g r) -> q g r", r=PACK),
                     ACT.Exp,
                     bias=neg_max[b][:],
                     scale=-1.0,
                     accum_out=page_sums[b][:, h : h + 1],
                 )
-                turned[page] = turn.tile([P, PACK * P], F32, name="turned")
-                for t in range(PACK):
-                    place = turned[page][:, t * P : (t + 1) * P] if b else turned[page][:, t :: PACK]
-                    nc.tensor.transpose(place, p_sb[b][:, h, t, :], ident[:])
+                turned[page] = turn.tile([P, PACK * NQ], F32, name="turned")
+                for r in range(PACK):
+                    place = turned[page][:, r * NQ : (r + 1) * NQ] if b else turned[page][:, r::PACK]
+                    nc.tensor.transpose(place, p_sb[b][:, h, r, :], ident[:])
 
-        def weigh_on_vector(page):
-            nc.vector.tensor_tensor(
-                w_bf[page // SEQ_PAGES][:, page % SEQ_PAGES, :, :],
-                turned[page][:].rearrange("s (q t) -> s q t", t=PACK),
-                vs_turned[0][:, page, 0:PACK].unsqueeze(1).to_broadcast([P, NQ, PACK]),
-                ALU.mult,
-            )
-
-        def scale_on_scalar(page):
-            planes[page] = reused.tile([P, PACK, NQ], BF16, name=f"planes{page}", tag=f"scores{PAGES + SEQ_PAGES - 1 - page}", align_bytes=64)
-            for t in range(PACK):
-                nc.scalar.activation(planes[page][:, t, :], turned[page][:, t * P : (t + 1) * P], ACT.Copy, scale=vs_turned[1][:, page - SEQ_PAGES, t : t + 1])
-
-        def interleave_on_scalar(page):
-            nc.scalar.copy(w_bf[page // SEQ_PAGES][:, page % SEQ_PAGES, :, :], planes[page][:].rearrange("s t q -> s q t"))
-
-        def multiply(page):
-            b, h = divmod(page, SEQ_PAGES)
-            nc.vector.quantize_mx(
-                out=w_codes[b][:, h, :].bitcast(FP8X4), scales=w_scales[page][:], in_=w_bf[b][:, h, :, :].rearrange("s q t -> s (q t)")
-            )
-            first = b not in sums
-            if first:
-                sums[b] = acc.tile([P, DV], F32, name="sums", tag="acc")
-            cols = slice(page * DV, (page + 1) * DV)
-            nc.tensor.matmul_mx(
-                out=sums[b][:],
-                lhsT=w_codes[b][:, h, :].bitcast(FP8X4),
-                lhsT_scale=w_scales[page][:],
-                rhs=v_word_slots[page].bitcast(FP8X4),
-                rhs_scale=v_scale_slots[V_SCALE_ROW:P, cols],
-                start=first,
-                stop=not first,
-            )
-
-        def finish(b):
-            result = reused.tile([P, DV], F32, name=f"result{b}", tag="result" if b else "last", align_bytes=64)
-            nc.vector.scalar_tensor_tensor(result[:], sums[b][:], inverses[:, b : b + 1], gate[:, b * DV : (b + 1) * DV], ALU.mult, ALU.mult)
-            nc.sync.dma_start(out[b], result[:])
-
-        for page in range(PAGES):
-            gather_keys(page)
+        for page in range(LAST):
             score(page)
-        for h in range(SEQ_PAGES):
-            for b in range(B):
-                row_max(b * SEQ_PAGES + h)
-        for b in range(B):
-            exponentials(b)
+        row_max(0)
+        score(LAST)
+        row_max(1)
+        exponentials(0)
+        row_max(2)
+        gather_vs(reused.tile([P, PAGE], F32, name="vs_slots_page0", tag="keys0", align_bytes=64), 0, 1)
+        row_max(LAST)
+        exponentials(1)
 
         def gather_values(slots, first, count):
             nc.vector.tensor_copy(slots[:], v_word_pool[:].bitcast(U32).indirect(entries(column_list, first * DV, count * DV)))
             for e in range(count):
                 v_word_slots[first + e] = slots[:, e * DV : (e + 1) * DV]
 
-        gather_vs(late.tile([P, PAGE], F32, name="vs_slots_first", offset=0, align_bytes=64), 0, 1)
-        v_word_slots = {}
-        v_scale_slots = reused.tile([P, PAGES * DV], U8, name="v_scale_slots", tag=f"page{PAGES - 2}", align_bytes=64)
+        v_scale_slots = late.tile([P, PAGES * DV], U8, name="v_scale_slots", offset=V_SCALE_SLOTS_AT, align_bytes=64)
         nc.vector.tensor_copy(v_scale_slots[:], v_scale_pool[:].bitcast(U8).indirect(column_list[:]))
-        gather_values(late.tile([P, (PAGES - 1) * DV], U32, name="v_word_slots", offset=2048, align_bytes=64), 0, PAGES - 1)
+        gather_values(late.tile([P, LAST * DV], U32, name="v_word_slots", offset=V_WORD_SLOTS_AT, align_bytes=64), 0, LAST)
 
         w_bf = [
-            after_cast.tile([P, SEQ_PAGES, NQ, PACK], BF16, name="w_bf0", offset=16384, align_bytes=64),
-            reused.tile([P, SEQ_PAGES, NQ, PACK], BF16, name="w_bf1", tag="last", align_bytes=64),
+            staged.tile([P, SEQ_PAGES, NQ, PACK], BF16, name="w_bf0", offset=P_AT[1], align_bytes=64),
+            reused.tile([P, SEQ_PAGES, NQ, PACK], BF16, name="w_bf1", tag="last_weights", align_bytes=64),
         ]
         w_codes = [held.tile([P, SEQ_PAGES, NQ], U32, name=f"w_codes{b}", align_bytes=64) for b in range(B)]
         inverses = held.tile([P, B], F32, name="inverses")
 
-        for page in (2, 3):
-            scale_on_scalar(page)
-        for page in (2, 3):
-            interleave_on_scalar(page)
+        for h in range(SEQ_PAGES):
+            page = SEQ_PAGES + h
+            planes[h] = reused.tile([P, PACK, NQ], BF16, name=f"planes{h}", tag=f"scores{LAST - h}", align_bytes=64)
+            for r in range(PACK):
+                nc.scalar.activation(planes[h][:, r, :], turned[page][:, r * NQ : (r + 1) * NQ], ACT.Copy, scale=vs_turned[1][:, h, r : r + 1])
+        for h in range(SEQ_PAGES):
+            nc.scalar.copy(w_bf[1][:, h, :, :], planes[h][:].rearrange("g r q -> g q r"))
         for b in range(B):
             nc.scalar.activation(totals[:, b : b + 1], page_sums[b][:, 0:1], ACT.Identity, bias=page_sums[b][:, 1:2], scale=1.0)
-        weigh_on_vector(1)
-        weigh_on_vector(0)
+
+        for h in reversed(range(SEQ_PAGES)):
+            nc.vector.tensor_tensor(
+                w_bf[0][:, h, :, :],
+                turned[h][:].rearrange("g (q r) -> g q r", r=PACK),
+                vs_turned[0][:, h, 0:PACK].unsqueeze(1).to_broadcast([P, NQ, PACK]),
+                ALU.mult,
+            )
+
+        parts = (1, 2)
+
+        def multiply(page):
+            b, h = divmod(page, SEQ_PAGES)
+            nc.vector.quantize_mx(
+                out=w_codes[b][:, h, :].bitcast(FP8X4), scales=w_scales[page][:], in_=w_bf[b][:, h, :, :].rearrange("g q r -> g (q r)")
+            )
+            opens = b not in sums
+            width = DV // parts[b]
+            if opens:
+                sums[b] = [acc.tile([P, width], F32, name="sums", tag="acc") for part in range(parts[b])]
+            for part in range(parts[b]):
+                nc.tensor.matmul_mx(
+                    out=sums[b][part][:],
+                    lhsT=w_codes[b][:, h, :].bitcast(FP8X4),
+                    lhsT_scale=w_scales[page][:],
+                    rhs=v_word_slots[page][:, part * width : (part + 1) * width].bitcast(FP8X4),
+                    rhs_scale=v_scale_slots[V_SCALE_ROW:P, page * DV + part * width : page * DV + (part + 1) * width],
+                    start=opens,
+                    stop=not opens,
+                )
+
+        def finish(b, result):
+            width = DV // parts[b]
+            for part in range(parts[b]):
+                nc.vector.scalar_tensor_tensor(
+                    result[:, part * width : (part + 1) * width],
+                    sums[b][part][:],
+                    inverses[:, b : b + 1],
+                    gate[:, b * DV + part * width : b * DV + (part + 1) * width],
+                    ALU.mult,
+                    ALU.mult,
+                )
+            nc.sync.dma_start(out[b], result[:])
+
         multiply(1)
         multiply(0)
         multiply(2)
-        gather_values(reused.tile([P, DV], U32, name="v_word_slots_last", tag="scores3", align_bytes=64), 3, 1)
-        multiply(3)
+        gather_values(reused.tile([P, DV], U32, name="v_word_slots_last", tag=f"scores{LAST}", align_bytes=64), LAST, 1)
+        multiply(LAST)
         nc.vector.reciprocal(inverses[:], totals[:])
-        finish(0)
-        finish(1)
+        finish(0, reused.tile([P, DV], F32, name="result0", tag="last_weights", align_bytes=64))
+        finish(1, reused.tile([P, DV], F32, name="result1", tag="result1", align_bytes=64))

@@ -15,12 +15,7 @@ GROUP = 16
 QUADRANT = 32
 VS_ROW = P - 1
 V_SCALE_ROW = 4
-VS_PITCH = 2 * PACK
 
-Q_RAW_BYTES = PACK * NQ * 4
-Q_RAW_AT = (0, Q_RAW_BYTES)
-P_BYTES = SEQ_PAGES * PAGE * 4
-P_AT = (B * Q_RAW_BYTES, B * Q_RAW_BYTES + P_BYTES)
 V_SCALE_SLOTS_AT = 0
 NEG_SCORES1_AT = V_SCALE_SLOTS_AT + PAGES * DV // 2
 V_WORD_SLOTS_AT = V_SCALE_SLOTS_AT + PAGES * DV
@@ -42,7 +37,6 @@ def tile_attend_pkv8_gate_kernel(tc, qT, k_words, k_scales, v_words, v_scales, v
     nc = tc.nc
     with ExitStack() as ctx:
         held = ctx.enter_context(tc.tile_pool(name="held", bufs=1))
-        staged = ctx.enter_context(tc.tile_pool(name="staged", bufs=1))
         reused = ctx.enter_context(tc.tile_pool(name="reused", bufs=1))
         late = ctx.enter_context(tc.tile_pool(name="late", bufs=1))
         acc = ctx.enter_context(tc.psum_pool(name="acc", bufs=PAGES))
@@ -55,10 +49,8 @@ def tile_attend_pkv8_gate_kernel(tc, qT, k_words, k_scales, v_words, v_scales, v
         nc.sync.dma_start(slot_list[:], offs)
         vs_pool = held.tile([P, T], F32, name="vs_pool")
         nc.sync.dma_start(vs_pool[VS_ROW : VS_ROW + 1, :], vs[0:1, :])
-        q_raw = [staged.tile([P, PACK, NQ], F32, name=f"q_raw{b}", offset=Q_RAW_AT[b]) for b in range(B)]
+        q_raw = [reused.tile([P, PACK, NQ], F32, name=f"q_raw{b}", tag=f"q_raw{b}") for b in range(B)]
         nc.sync.dma_start(q_raw[0][:], qT[0].rearrange("(g r) q -> g r q", r=PACK))
-        column_list = held.tile([P, PAGES * DV // GROUP], U16, name="column_list")
-        nc.sync.dma_start(column_list[:], voffs)
 
         k_scale_pool = held.tile([P, T // 4], I32, name="k_scale_pool")
         nc.vector.memset(k_scale_pool[:], 0)
@@ -71,30 +63,14 @@ def tile_attend_pkv8_gate_kernel(tc, qT, k_words, k_scales, v_words, v_scales, v
         nc.sync.dma_start(q_raw[1][:], qT[1].rearrange("(g r) q -> g r q", r=PACK))
         og_sb = held.tile([P, B, DV], F32, name="og_sb")
         nc.sync.dma_start(og_sb[:], og.rearrange("b q e -> q b e"))
-        v_word_pool = held.tile([P, POOL_PAGES * DV], I32, name="v_word_pool")
-        nc.sync.dma_start(
-            v_word_pool[:].rearrange("g (u e) -> g u e", u=POOL_PAGES),
-            v_words.rearrange("u g e r -> g u (e r)").bitcast(I32),
-        )
+        column_list = held.tile([P, PAGES * DV // GROUP], U16, name="column_list")
+        nc.sync.dma_start(column_list[:], voffs)
 
         ident = held.tile([P, P], F32, name="ident")
         make_identity(nc, ident[:])
 
-        vs_turned = [held.tile([P, SEQ_PAGES, VS_PITCH], F32, name=f"vs_turned{b}") for b in range(B)]
-
-        def gather_vs(slots, first, count):
-            nc.vector.tensor_copy(slots[:], vs_pool[:].indirect(entries(slot_list, first * PAGE, count * PAGE)))
-            for e in range(count):
-                b, h = divmod(first + e, SEQ_PAGES)
-                nc.sync.dma_start(
-                    vs_turned[b][:, h, 0:PACK],
-                    slots[VS_ROW : VS_ROW + 1, e * PAGE : (e + 1) * PAGE].rearrange("o (g r) -> o g r", r=PACK),
-                )
-
-        gather_vs(held.tile([P, LAST * PAGE], F32, name="vs_slots"), 1, LAST)
-
-        k_scale_slots = held.tile([P, B * N], U8, name="k_scale_slots", align_bytes=64)
-        nc.vector.tensor_copy(k_scale_slots[:], k_scale_pool[:].bitcast(U8).indirect(slot_list[:]))
+        vs_slots = held.tile([P, PAGES * PAGE], F32, name="vs_slots")
+        nc.vector.tensor_copy(vs_slots[:], vs_pool[:].indirect(slot_list[:]))
 
         q_bf = [held.tile([P, NQ, PACK], BF16, name=f"q_bf{b}", align_bytes=64) for b in range(B)]
         q_codes = [held.tile([P, NQ], U32, name=f"q_codes{b}", align_bytes=64) for b in range(B)]
@@ -103,36 +79,49 @@ def tile_attend_pkv8_gate_kernel(tc, qT, k_words, k_scales, v_words, v_scales, v
             nc.scalar.activation(q_bf[b][:], q_raw[b][:].rearrange("g r q -> g q r"), ACT.Copy)
             nc.vector.quantize_mx(out=q_codes[b][:].bitcast(FP8X4), scales=q_scales[b][:], in_=q_bf[b][:].rearrange("g q r -> g (q r)"))
 
-        v_scale_pool = staged.tile([P, POOL_PAGES * DV // 4], I32, name="v_scale_pool", offset=Q_RAW_AT[1])
+        k_scale_slots = held.tile([P, B * N], U8, name="k_scale_slots", align_bytes=64)
+        nc.vector.tensor_copy(k_scale_slots[:], k_scale_pool[:].bitcast(U8).indirect(slot_list[:]))
+
+        v_scale_pool = reused.tile([P, POOL_PAGES * DV // 4], I32, name="v_scale_pool", tag="q_raw0")
         nc.gpsimd.memset(v_scale_pool[:], 0)
         v_scale_rows = v_scales.rearrange("u f e -> f u e").bitcast(I32)
         for j in range(4):
-            nc.scalar.dma_start(
+            nc.sync.dma_start(
                 v_scale_pool[V_SCALE_ROW + j : P : QUADRANT, :].rearrange("f (u e) -> f u e", u=POOL_PAGES),
                 v_scale_rows[j:16:4, :, :],
             )
+        v_word_pool = held.tile([P, POOL_PAGES * DV], I32, name="v_word_pool")
+        nc.sync.dma_start(
+            v_word_pool[:].rearrange("g (u e) -> g u e", u=POOL_PAGES),
+            v_words.rearrange("u g e r -> g u (e r)").bitcast(I32),
+        )
+        vs_turned = [reused.tile([P, PACK], F32, name=f"vs_turned{page}", tag=f"vs_turned{page}") for page in range(PAGES)]
+        for page in range(PAGES):
+            nc.sync.dma_start(
+                vs_turned[page][:],
+                vs_slots[VS_ROW : VS_ROW + 1, page * PAGE : (page + 1) * PAGE].rearrange("o (g r) -> o g r", r=PACK),
+            )
 
-        half_tanh = staged.tile([P, B * DV], F32, name="half_tanh", offset=P_AT[0])
+        half_tanh = held.tile([P, B * DV], F32, name="half_tanh")
         nc.scalar.activation(half_tanh[:], og_sb[:].rearrange("q b e -> q (b e)"), ACT.Tanh, scale=0.5)
         gate = held.tile([P, B * DV], F32, name="gate")
         nc.scalar.activation(gate[:], half_tanh[:], ACT.Copy, bias=0.5, scale=0.5)
 
         neg_scores = [
-            late.tile([P, PAGE], F32, name="neg_scores1", offset=NEG_SCORES1_AT, align_bytes=64)
+            late.tile([P, PACK, P], F32, name="neg_scores1", offset=NEG_SCORES1_AT, align_bytes=64)
             if page == SEQ_PAGES - 1
-            else reused.tile([P, PAGE], F32, name=f"neg_scores{page}", tag=f"scores{page}", align_bytes=64)
+            else held.tile([P, PACK, P], F32, name=f"neg_scores{page}", align_bytes=64)
             for page in range(PAGES)
         ]
         first_neg_max = [held.tile([P, 1], F32, name=f"first_neg_max{b}") for b in range(B)]
         neg_max = [held.tile([P, 1], F32, name=f"neg_max{b}") for b in range(B)]
         page_sums = [held.tile([P, SEQ_PAGES], F32, name=f"page_sums{b}") for b in range(B)]
-        totals = held.tile([P, B], F32, name="totals")
-        p_sb = [staged.tile([P, SEQ_PAGES, PACK, P], F32, name=f"p_sb{b}", offset=P_AT[b]) for b in range(B)]
+        p_sb = [held.tile([P, PACK, P], F32, name=f"p_sb{page}") for page in range(PAGES)]
         w_scales = [held.tile([P, NQ], U8, name=f"w_scales{page}", align_bytes=64) for page in range(PAGES)]
+        w_codes = [held.tile([P, NQ], U32, name=f"w_codes{page}", align_bytes=64) for page in range(PAGES)]
+        w_bf = [held.tile([P, NQ, PACK], BF16, name=f"w_bf{page}", align_bytes=64) for page in range(PAGES)]
         scores = {}
         turned = {}
-        planes = {}
-        v_word_slots = {}
         sums = {}
 
         def score(page):
@@ -154,7 +143,7 @@ def tile_attend_pkv8_gate_kernel(tc, qT, k_words, k_scales, v_words, v_scales, v
             b, h = divmod(page, SEQ_PAGES)
             nc.vector.tensor_scalar(
                 neg_scores[page][:],
-                scores[page][:],
+                scores[page][:].rearrange("q (g r) -> q r g", r=PACK),
                 -1.0,
                 first_neg_max[b][:] if h else None,
                 ALU.mult,
@@ -166,17 +155,11 @@ def tile_attend_pkv8_gate_kernel(tc, qT, k_words, k_scales, v_words, v_scales, v
             for h in range(SEQ_PAGES):
                 page = b * SEQ_PAGES + h
                 nc.scalar.activation(
-                    p_sb[b][:, h, :, :].rearrange("q r g -> q g r"),
-                    neg_scores[page][:].rearrange("q (g r) -> q g r", r=PACK),
-                    ACT.Exp,
-                    bias=neg_max[b][:],
-                    scale=-1.0,
-                    accum_out=page_sums[b][:, h : h + 1],
+                    p_sb[page][:], neg_scores[page][:], ACT.Exp, bias=neg_max[b][:], scale=-1.0, accum_out=page_sums[b][:, h : h + 1]
                 )
-                turned[page] = turn.tile([P, PACK * NQ], F32, name="turned")
+                turned[page] = turn.tile([P, PACK, NQ], F32, name="turned")
                 for r in range(PACK):
-                    place = turned[page][:, r * NQ : (r + 1) * NQ] if b else turned[page][:, r::PACK]
-                    nc.tensor.transpose(place, p_sb[b][:, h, r, :], ident[:])
+                    nc.tensor.transpose(turned[page][:, r, :], p_sb[page][:, r, :], ident[:])
 
         for page in range(LAST):
             score(page)
@@ -185,67 +168,58 @@ def tile_attend_pkv8_gate_kernel(tc, qT, k_words, k_scales, v_words, v_scales, v
         row_max(1)
         exponentials(0)
         row_max(2)
-        gather_vs(reused.tile([P, PAGE], F32, name="vs_slots_page0", tag="keys0", align_bytes=64), 0, 1)
+        first_v_scales = held.tile([P, DV], U8, name="first_v_scales", align_bytes=64)
+        nc.vector.tensor_copy(first_v_scales[:], v_scale_pool[:].bitcast(U8).indirect(entries(column_list, 0, DV)))
         row_max(LAST)
         exponentials(1)
 
-        def gather_values(slots, first, count):
-            nc.vector.tensor_copy(slots[:], v_word_pool[:].bitcast(U32).indirect(entries(column_list, first * DV, count * DV)))
-            for e in range(count):
-                v_word_slots[first + e] = slots[:, e * DV : (e + 1) * DV]
+        other_v_scales = late.tile([P, LAST * DV], U8, name="other_v_scales", offset=V_SCALE_SLOTS_AT, align_bytes=64)
+        nc.vector.tensor_copy(other_v_scales[:], v_scale_pool[:].bitcast(U8).indirect(entries(column_list, DV, LAST * DV)))
+        v_word_slots = late.tile([P, PAGES * DV], U32, name="v_word_slots", offset=V_WORD_SLOTS_AT, align_bytes=64)
+        nc.vector.tensor_copy(v_word_slots[:], v_word_pool[:].bitcast(U32).indirect(column_list[:]))
 
-        v_scale_slots = late.tile([P, PAGES * DV], U8, name="v_scale_slots", offset=V_SCALE_SLOTS_AT, align_bytes=64)
-        nc.vector.tensor_copy(v_scale_slots[:], v_scale_pool[:].bitcast(U8).indirect(column_list[:]))
-        gather_values(late.tile([P, LAST * DV], U32, name="v_word_slots", offset=V_WORD_SLOTS_AT, align_bytes=64), 0, LAST)
-
-        w_bf = [
-            staged.tile([P, SEQ_PAGES, NQ, PACK], BF16, name="w_bf0", offset=P_AT[1], align_bytes=64),
-            reused.tile([P, SEQ_PAGES, NQ, PACK], BF16, name="w_bf1", tag="last_weights", align_bytes=64),
-        ]
-        w_codes = [held.tile([P, SEQ_PAGES, NQ], U32, name=f"w_codes{b}", align_bytes=64) for b in range(B)]
-        inverses = held.tile([P, B], F32, name="inverses")
-
-        for h in range(SEQ_PAGES):
-            page = SEQ_PAGES + h
-            planes[h] = reused.tile([P, PACK, NQ], BF16, name=f"planes{h}", tag=f"scores{LAST - h}", align_bytes=64)
-            for r in range(PACK):
-                nc.scalar.activation(planes[h][:, r, :], turned[page][:, r * NQ : (r + 1) * NQ], ACT.Copy, scale=vs_turned[1][:, h, r : r + 1])
-        for h in range(SEQ_PAGES):
-            nc.scalar.copy(w_bf[1][:, h, :, :], planes[h][:].rearrange("g r q -> g q r"))
+        totals = held.tile([P, B], F32, name="totals")
         for b in range(B):
-            nc.scalar.activation(totals[:, b : b + 1], page_sums[b][:, 0:1], ACT.Identity, bias=page_sums[b][:, 1:2], scale=1.0)
+            nc.gpsimd.tensor_tensor(totals[:, b : b + 1], page_sums[b][:, 0:1], page_sums[b][:, 1:2], ALU.add)
 
-        for h in reversed(range(SEQ_PAGES)):
+        def weigh_on_scalar(page):
+            planes = held.tile([P, PACK, NQ], BF16, name=f"planes{page}", align_bytes=64)
+            for r in range(PACK):
+                nc.scalar.activation(planes[:, r, :], turned[page][:, r, :], ACT.Copy, scale=vs_turned[page][:, r : r + 1])
+            nc.scalar.copy(
+                w_bf[page][:].rearrange("g (c i) r -> g c r i", i=PACK), planes[:].rearrange("g r (c i) -> g c r i", i=PACK)
+            )
+
+        def weigh_on_vector(page):
             nc.vector.tensor_tensor(
-                w_bf[0][:, h, :, :],
-                turned[h][:].rearrange("g (q r) -> g q r", r=PACK),
-                vs_turned[0][:, h, 0:PACK].unsqueeze(1).to_broadcast([P, NQ, PACK]),
+                w_bf[page][:],
+                turned[page][:].rearrange("g r q -> g q r"),
+                vs_turned[page][:].unsqueeze(1).to_broadcast([P, NQ, PACK]),
                 ALU.mult,
             )
 
-        parts = (1, 2)
+        parts = (2, 1)
 
         def multiply(page):
             b, h = divmod(page, SEQ_PAGES)
-            nc.vector.quantize_mx(
-                out=w_codes[b][:, h, :].bitcast(FP8X4), scales=w_scales[page][:], in_=w_bf[b][:, h, :, :].rearrange("g q r -> g (q r)")
-            )
-            opens = b not in sums
+            nc.vector.quantize_mx(out=w_codes[page][:].bitcast(FP8X4), scales=w_scales[page][:], in_=w_bf[page][:].rearrange("g q r -> g (q r)"))
             width = DV // parts[b]
-            if opens:
+            if h == 0:
                 sums[b] = [acc.tile([P, width], F32, name="sums", tag="acc") for part in range(parts[b])]
             for part in range(parts[b]):
+                at = page * DV + part * width
                 nc.tensor.matmul_mx(
                     out=sums[b][part][:],
-                    lhsT=w_codes[b][:, h, :].bitcast(FP8X4),
+                    lhsT=w_codes[page][:].bitcast(FP8X4),
                     lhsT_scale=w_scales[page][:],
-                    rhs=v_word_slots[page][:, part * width : (part + 1) * width].bitcast(FP8X4),
-                    rhs_scale=v_scale_slots[V_SCALE_ROW:P, page * DV + part * width : page * DV + (part + 1) * width],
-                    start=opens,
-                    stop=not opens,
+                    rhs=v_word_slots[:, at : at + width].bitcast(FP8X4),
+                    rhs_scale=other_v_scales[V_SCALE_ROW:P, at - DV : at - DV + width] if page else first_v_scales[V_SCALE_ROW:P, at : at + width],
+                    start=h == 0,
+                    stop=h == SEQ_PAGES - 1,
                 )
 
-        def finish(b, result):
+        def finish(b):
+            result = held.tile([P, DV], F32, name=f"result{b}")
             width = DV // parts[b]
             for part in range(parts[b]):
                 nc.vector.scalar_tensor_tensor(
@@ -258,11 +232,15 @@ def tile_attend_pkv8_gate_kernel(tc, qT, k_words, k_scales, v_words, v_scales, v
                 )
             nc.sync.dma_start(out[b], result[:])
 
-        multiply(1)
+        weigh_on_scalar(0)
+        weigh_on_scalar(1)
+        weigh_on_vector(2)
         multiply(0)
+        weigh_on_vector(3)
         multiply(2)
-        gather_values(reused.tile([P, DV], U32, name="v_word_slots_last", tag=f"scores{LAST}", align_bytes=64), LAST, 1)
-        multiply(LAST)
+        multiply(3)
+        inverses = reused.tile([P, B], F32, name="inverses", tag="vs_turned2")
         nc.vector.reciprocal(inverses[:], totals[:])
-        finish(0, reused.tile([P, DV], F32, name="result0", tag="last_weights", align_bytes=64))
-        finish(1, reused.tile([P, DV], F32, name="result1", tag="result1", align_bytes=64))
+        multiply(1)
+        finish(1)
+        finish(0)

@@ -20,6 +20,10 @@ V_SCALE_SLOTS_AT = 0
 NEG_SCORES1_AT = V_SCALE_SLOTS_AT + PAGES * DV // 2
 V_WORD_SLOTS_AT = V_SCALE_SLOTS_AT + PAGES * DV
 
+IDENT_AT = 0
+FIRST_KEYS_AT = IDENT_AT + P * 4 - 64
+LAST_KEYS_AT = IDENT_AT + P * 4
+
 FLOPS = 2 * B * NQ * N * (D + DV)
 
 F32 = mybir.dt.float32
@@ -39,16 +43,17 @@ def tile_attend_pkv8_gate_kernel(tc, qT, k_words, k_scales, v_words, v_scales, v
         held = ctx.enter_context(tc.tile_pool(name="held", bufs=1))
         reused = ctx.enter_context(tc.tile_pool(name="reused", bufs=1))
         late = ctx.enter_context(tc.tile_pool(name="late", bufs=1))
+        relay = ctx.enter_context(tc.tile_pool(name="relay", bufs=1))
         acc = ctx.enter_context(tc.psum_pool(name="acc", bufs=PAGES))
         turn = ctx.enter_context(tc.psum_pool(name="turn", bufs=PAGES))
 
         def entries(index_list, first, count):
             return index_list[:, first // GROUP : (first + count) // GROUP]
 
-        slot_list = held.tile([P, B * N // GROUP], U16, name="slot_list")
-        nc.sync.dma_start(slot_list[:], offs)
         vs_pool = held.tile([P, T], F32, name="vs_pool")
         nc.sync.dma_start(vs_pool[VS_ROW : VS_ROW + 1, :], vs[0:1, :])
+        slot_list = held.tile([P, B * N // GROUP], U16, name="slot_list")
+        nc.sync.dma_start(slot_list[:], offs)
         q_raw = [reused.tile([P, PACK, NQ], F32, name=f"q_raw{b}", tag=f"q_raw{b}") for b in range(B)]
         nc.sync.dma_start(q_raw[0][:], qT[0].rearrange("(g r) q -> g r q", r=PACK))
 
@@ -66,11 +71,8 @@ def tile_attend_pkv8_gate_kernel(tc, qT, k_words, k_scales, v_words, v_scales, v
         column_list = held.tile([P, PAGES * DV // GROUP], U16, name="column_list")
         nc.sync.dma_start(column_list[:], voffs)
 
-        ident = held.tile([P, P], F32, name="ident")
-        make_identity(nc, ident[:])
-
-        vs_slots = held.tile([P, PAGES * PAGE], F32, name="vs_slots")
-        nc.vector.tensor_copy(vs_slots[:], vs_pool[:].indirect(slot_list[:]))
+        vs_slots = held.tile([P, LAST * PAGE], F32, name="vs_slots")
+        nc.vector.tensor_copy(vs_slots[:], vs_pool[:].indirect(entries(slot_list, 0, LAST * PAGE)))
 
         q_bf = [held.tile([P, NQ, PACK], BF16, name=f"q_bf{b}", align_bytes=64) for b in range(B)]
         q_codes = [held.tile([P, NQ], U32, name=f"q_codes{b}", align_bytes=64) for b in range(B)]
@@ -95,12 +97,13 @@ def tile_attend_pkv8_gate_kernel(tc, qT, k_words, k_scales, v_words, v_scales, v
             v_word_pool[:].rearrange("g (u e) -> g u e", u=POOL_PAGES),
             v_words.rearrange("u g e r -> g u (e r)").bitcast(I32),
         )
-        vs_turned = [reused.tile([P, PACK], F32, name=f"vs_turned{page}", tag=f"vs_turned{page}") for page in range(PAGES)]
-        for page in range(PAGES):
-            nc.sync.dma_start(
-                vs_turned[page][:],
-                vs_slots[VS_ROW : VS_ROW + 1, page * PAGE : (page + 1) * PAGE].rearrange("o (g r) -> o g r", r=PACK),
-            )
+        vs_turned = [reused.tile([P, PACK], F32, name=f"vs_turned{page}", tag=f"vs_turned{page}", align_bytes=64) for page in range(PAGES)]
+
+        def turn_vs(page, slots):
+            nc.sync.dma_start(vs_turned[page][:], slots[VS_ROW : VS_ROW + 1, :].rearrange("o (g r) -> o g r", r=PACK))
+
+        for page in range(LAST):
+            turn_vs(page, vs_slots[:, page * PAGE : (page + 1) * PAGE])
 
         half_tanh = held.tile([P, B * DV], F32, name="half_tanh")
         nc.scalar.activation(half_tanh[:], og_sb[:].rearrange("q b e -> q (b e)"), ACT.Tanh, scale=0.5)
@@ -108,10 +111,8 @@ def tile_attend_pkv8_gate_kernel(tc, qT, k_words, k_scales, v_words, v_scales, v
         nc.scalar.activation(gate[:], half_tanh[:], ACT.Copy, bias=0.5, scale=0.5)
 
         neg_scores = [
-            late.tile([P, PACK, P], F32, name="neg_scores1", offset=NEG_SCORES1_AT, align_bytes=64)
-            if page == SEQ_PAGES - 1
-            else held.tile([P, PACK, P], F32, name=f"neg_scores{page}", align_bytes=64)
-            for page in range(PAGES)
+            late.tile([P, PACK, P], F32, name="neg_scores0", offset=NEG_SCORES1_AT, align_bytes=64),
+            held.tile([P, PACK, P], F32, name="neg_scores1", align_bytes=64),
         ]
         first_neg_max = [held.tile([P, 1], F32, name=f"first_neg_max{b}") for b in range(B)]
         neg_max = [held.tile([P, 1], F32, name=f"neg_max{b}") for b in range(B)]
@@ -119,14 +120,17 @@ def tile_attend_pkv8_gate_kernel(tc, qT, k_words, k_scales, v_words, v_scales, v
         p_sb = [held.tile([P, PACK, P], F32, name=f"p_sb{page}") for page in range(PAGES)]
         w_scales = [held.tile([P, NQ], U8, name=f"w_scales{page}", align_bytes=64) for page in range(PAGES)]
         w_codes = [held.tile([P, NQ], U32, name=f"w_codes{page}", align_bytes=64) for page in range(PAGES)]
-        w_bf = [held.tile([P, NQ, PACK], BF16, name=f"w_bf{page}", align_bytes=64) for page in range(PAGES)]
+        w_bf = [reused.tile([P, NQ, PACK], BF16, name=f"w_bf{page}", tag=f"w_bf{page}", align_bytes=64) for page in range(PAGES)]
         scores = {}
         turned = {}
         sums = {}
 
         def score(page):
             b = page // SEQ_PAGES
-            keys = reused.tile([P, PAGE], U32, name=f"k_word_slots{page}", tag=f"keys{page % LAST}", align_bytes=64)
+            if page in (0, LAST):
+                keys = relay.tile([P, PAGE], U32, name=f"k_word_slots{page}", offset=LAST_KEYS_AT if page else FIRST_KEYS_AT, align_bytes=64)
+            else:
+                keys = held.tile([P, PAGE], U32, name=f"k_word_slots{page}", align_bytes=64)
             nc.vector.tensor_copy(keys[:], k_word_pool[:].bitcast(U32).indirect(entries(slot_list, page * PAGE, PAGE)))
             scores[page] = acc.tile([P, PAGE], F32, name="score", tag="acc")
             nc.tensor.matmul_mx(
@@ -139,23 +143,26 @@ def tile_attend_pkv8_gate_kernel(tc, qT, k_words, k_scales, v_words, v_scales, v
                 stop=True,
             )
 
+        def dealt(page):
+            return scores[page][:].rearrange("q (g r) -> q r g", r=PACK)
+
         def row_max(page):
             b, h = divmod(page, SEQ_PAGES)
-            nc.vector.tensor_scalar(
-                neg_scores[page][:],
-                scores[page][:].rearrange("q (g r) -> q r g", r=PACK),
-                -1.0,
-                first_neg_max[b][:] if h else None,
-                ALU.mult,
-                ALU.min,
-                accum_out=neg_max[b][:] if h else first_neg_max[b][:],
-            )
+            if h == 0:
+                nc.vector.tensor_reduce(first_neg_max[b][:], scores[page][:], mybir.AxisListType.X, ALU.max, negate=True)
+            else:
+                nc.vector.tensor_scalar(neg_scores[b][:], dealt(page), -1.0, first_neg_max[b][:], ALU.mult, ALU.min, accum_out=neg_max[b][:])
 
         def exponentials(b):
             for h in range(SEQ_PAGES):
                 page = b * SEQ_PAGES + h
                 nc.scalar.activation(
-                    p_sb[page][:], neg_scores[page][:], ACT.Exp, bias=neg_max[b][:], scale=-1.0, accum_out=page_sums[b][:, h : h + 1]
+                    p_sb[page][:],
+                    neg_scores[b][:] if h else dealt(page),
+                    ACT.Exp,
+                    bias=neg_max[b][:],
+                    scale=-1.0 if h else 1.0,
+                    accum_out=page_sums[b][:, h : h + 1],
                 )
                 turned[page] = turn.tile([P, PACK, NQ], F32, name="turned")
                 for r in range(PACK):
@@ -163,27 +170,32 @@ def tile_attend_pkv8_gate_kernel(tc, qT, k_words, k_scales, v_words, v_scales, v
 
         for page in range(LAST):
             score(page)
+        ident = relay.tile([P, P], F32, name="ident", offset=IDENT_AT, align_bytes=64)
+        make_identity(nc, ident[:])
         row_max(0)
         score(LAST)
         row_max(1)
         exponentials(0)
         row_max(2)
-        first_v_scales = held.tile([P, DV], U8, name="first_v_scales", align_bytes=64)
-        nc.vector.tensor_copy(first_v_scales[:], v_scale_pool[:].bitcast(U8).indirect(entries(column_list, 0, DV)))
+        last_vs_slots = relay.tile([P, PAGE], F32, name="last_vs_slots", offset=LAST_KEYS_AT, align_bytes=64)
+        nc.vector.tensor_copy(last_vs_slots[:], vs_pool[:].indirect(entries(slot_list, LAST * PAGE, PAGE)))
+        turn_vs(LAST, last_vs_slots[:, :])
         row_max(LAST)
         exponentials(1)
 
-        other_v_scales = late.tile([P, LAST * DV], U8, name="other_v_scales", offset=V_SCALE_SLOTS_AT, align_bytes=64)
-        nc.vector.tensor_copy(other_v_scales[:], v_scale_pool[:].bitcast(U8).indirect(entries(column_list, DV, LAST * DV)))
-        v_word_slots = late.tile([P, PAGES * DV], U32, name="v_word_slots", offset=V_WORD_SLOTS_AT, align_bytes=64)
-        nc.vector.tensor_copy(v_word_slots[:], v_word_pool[:].bitcast(U32).indirect(column_list[:]))
+        v_scale_slots = late.tile([P, PAGES * DV], U8, name="v_scale_slots", offset=V_SCALE_SLOTS_AT, align_bytes=64)
+        nc.vector.tensor_copy(v_scale_slots[:], v_scale_pool[:].bitcast(U8).indirect(column_list[:]))
+        v_word_slots = {}
 
-        totals = held.tile([P, B], F32, name="totals")
-        for b in range(B):
-            nc.gpsimd.tensor_tensor(totals[:, b : b + 1], page_sums[b][:, 0:1], page_sums[b][:, 1:2], ALU.add)
+        def gather_values(slots, first, count):
+            nc.vector.tensor_copy(slots[:], v_word_pool[:].bitcast(U32).indirect(entries(column_list, first * DV, count * DV)))
+            for e in range(count):
+                v_word_slots[first + e] = slots[:, e * DV : (e + 1) * DV]
+
+        gather_values(late.tile([P, SEQ_PAGES * DV], U32, name="v_word_slots1", offset=V_WORD_SLOTS_AT, align_bytes=64), SEQ_PAGES, SEQ_PAGES)
 
         def weigh_on_scalar(page):
-            planes = held.tile([P, PACK, NQ], BF16, name=f"planes{page}", align_bytes=64)
+            planes = reused.tile([P, PACK, NQ], BF16, name=f"planes{page}", tag=f"planes{page}", align_bytes=64)
             for r in range(PACK):
                 nc.scalar.activation(planes[:, r, :], turned[page][:, r, :], ACT.Copy, scale=vs_turned[page][:, r : r + 1])
             nc.scalar.copy(
@@ -200,9 +212,11 @@ def tile_attend_pkv8_gate_kernel(tc, qT, k_words, k_scales, v_words, v_scales, v
 
         parts = (2, 1)
 
+        def quantise(page):
+            nc.vector.quantize_mx(out=w_codes[page][:].bitcast(FP8X4), scales=w_scales[page][:], in_=w_bf[page][:].rearrange("g q r -> g (q r)"))
+
         def multiply(page):
             b, h = divmod(page, SEQ_PAGES)
-            nc.vector.quantize_mx(out=w_codes[page][:].bitcast(FP8X4), scales=w_scales[page][:], in_=w_bf[page][:].rearrange("g q r -> g (q r)"))
             width = DV // parts[b]
             if h == 0:
                 sums[b] = [acc.tile([P, width], F32, name="sums", tag="acc") for part in range(parts[b])]
@@ -212,8 +226,8 @@ def tile_attend_pkv8_gate_kernel(tc, qT, k_words, k_scales, v_words, v_scales, v
                     out=sums[b][part][:],
                     lhsT=w_codes[page][:].bitcast(FP8X4),
                     lhsT_scale=w_scales[page][:],
-                    rhs=v_word_slots[:, at : at + width].bitcast(FP8X4),
-                    rhs_scale=other_v_scales[V_SCALE_ROW:P, at - DV : at - DV + width] if page else first_v_scales[V_SCALE_ROW:P, at : at + width],
+                    rhs=v_word_slots[page][:, part * width : (part + 1) * width].bitcast(FP8X4),
+                    rhs_scale=v_scale_slots[V_SCALE_ROW:P, at : at + width],
                     start=h == 0,
                     stop=h == SEQ_PAGES - 1,
                 )
@@ -234,13 +248,21 @@ def tile_attend_pkv8_gate_kernel(tc, qT, k_words, k_scales, v_words, v_scales, v
 
         weigh_on_scalar(0)
         weigh_on_scalar(1)
+        totals = reused.tile([P, B], F32, name="totals", tag="planes0", align_bytes=64)
+        for b in range(B):
+            nc.scalar.activation(totals[:, b : b + 1], page_sums[b][:, 0:1], ACT.Identity, bias=page_sums[b][:, 1:2], scale=1.0)
         weigh_on_vector(2)
-        multiply(0)
         weigh_on_vector(3)
-        multiply(2)
-        multiply(3)
-        inverses = reused.tile([P, B], F32, name="inverses", tag="vs_turned2")
-        nc.vector.reciprocal(inverses[:], totals[:])
+        for page in (2, 3):
+            quantise(page)
+            multiply(page)
+        quantise(0)
+        gather_values(reused.tile([P, DV], U32, name="v_word_slots_page0", tag="vs_turned3", align_bytes=64), 0, 1)
+        multiply(0)
+        quantise(1)
+        gather_values(reused.tile([P, DV], U32, name="v_word_slots_page1", tag="planes1", align_bytes=64), 1, 1)
         multiply(1)
+        inverses = reused.tile([P, B], F32, name="inverses", tag="vs_turned2", align_bytes=64)
+        nc.vector.reciprocal(inverses[:], totals[:])
         finish(1)
         finish(0)

@@ -71,8 +71,8 @@ def tile_attend_pkv8_gate_kernel(tc, qT, k_words, k_scales, v_words, v_scales, v
         column_list = held.tile([P, PAGES * DV // GROUP], U16, name="column_list")
         nc.sync.dma_start(column_list[:], voffs)
 
-        vs_slots = held.tile([P, LAST * PAGE], F32, name="vs_slots")
-        nc.vector.tensor_copy(vs_slots[:], vs_pool[:].indirect(entries(slot_list, 0, LAST * PAGE)))
+        vs_slots = held.tile([P, PAGES * PAGE], F32, name="vs_slots")
+        nc.vector.tensor_copy(vs_slots[:], vs_pool[:].indirect(slot_list[:]))
 
         q_bf = [held.tile([P, NQ, PACK], BF16, name=f"q_bf{b}", align_bytes=64) for b in range(B)]
         q_codes = [held.tile([P, NQ], U32, name=f"q_codes{b}", align_bytes=64) for b in range(B)]
@@ -102,7 +102,7 @@ def tile_attend_pkv8_gate_kernel(tc, qT, k_words, k_scales, v_words, v_scales, v
         def turn_vs(page, slots):
             nc.sync.dma_start(vs_turned[page][:], slots[VS_ROW : VS_ROW + 1, :].rearrange("o (g r) -> o g r", r=PACK))
 
-        for page in range(LAST):
+        for page in range(PAGES):
             turn_vs(page, vs_slots[:, page * PAGE : (page + 1) * PAGE])
 
         half_tanh = held.tile([P, B * DV], F32, name="half_tanh")
@@ -177,9 +177,6 @@ def tile_attend_pkv8_gate_kernel(tc, qT, k_words, k_scales, v_words, v_scales, v
         row_max(1)
         exponentials(0)
         row_max(2)
-        last_vs_slots = relay.tile([P, PAGE], F32, name="last_vs_slots", offset=LAST_KEYS_AT, align_bytes=64)
-        nc.vector.tensor_copy(last_vs_slots[:], vs_pool[:].indirect(entries(slot_list, LAST * PAGE, PAGE)))
-        turn_vs(LAST, last_vs_slots[:, :])
         row_max(LAST)
         exponentials(1)
 
@@ -244,7 +241,7 @@ def tile_attend_pkv8_gate_kernel(tc, qT, k_words, k_scales, v_words, v_scales, v
                     ALU.mult,
                     ALU.mult,
                 )
-            nc.sync.dma_start(out[b], result[:])
+                nc.sync.dma_start(out[b][:, part * width : (part + 1) * width], result[:, part * width : (part + 1) * width])
 
         weigh_on_scalar(0)
         weigh_on_scalar(1)
@@ -259,8 +256,8 @@ def tile_attend_pkv8_gate_kernel(tc, qT, k_words, k_scales, v_words, v_scales, v
         quantise(0)
         gather_values(reused.tile([P, DV], U32, name="v_word_slots_page0", tag="vs_turned3", align_bytes=64), 0, 1)
         multiply(0)
+        gather_values(reused.tile([P, DV], U32, name="v_word_slots_page1", tag="w_bf2", align_bytes=64), 1, 1)
         quantise(1)
-        gather_values(reused.tile([P, DV], U32, name="v_word_slots_page1", tag="planes1", align_bytes=64), 1, 1)
         multiply(1)
         inverses = reused.tile([P, B], F32, name="inverses", tag="vs_turned2", align_bytes=64)
         nc.vector.reciprocal(inverses[:], totals[:])

@@ -13,16 +13,14 @@ LAST = PAGES - 1
 POOL_PAGES = T // PAGE
 GROUP = 16
 QUADRANT = 32
+RUN = 4
+SCALE_ROWS = PAGE // 32
 VS_ROW = P - 1
 V_SCALE_ROW = 4
 
-V_SCALE_SLOTS_AT = 0
-NEG_SCORES1_AT = V_SCALE_SLOTS_AT + PAGES * DV // 2
-V_WORD_SLOTS_AT = V_SCALE_SLOTS_AT + PAGES * DV
-
 IDENT_AT = 0
-FIRST_KEYS_AT = IDENT_AT + P * 4 - 64
 LAST_KEYS_AT = IDENT_AT + P * 4
+FIRST_KEYS_AT = LAST_KEYS_AT - 64
 
 FLOPS = 2 * B * NQ * N * (D + DV)
 
@@ -42,7 +40,6 @@ def tile_attend_pkv8_gate_kernel(tc, qT, k_words, k_scales, v_words, v_scales, v
     with ExitStack() as ctx:
         held = ctx.enter_context(tc.tile_pool(name="held", bufs=1))
         reused = ctx.enter_context(tc.tile_pool(name="reused", bufs=1))
-        late = ctx.enter_context(tc.tile_pool(name="late", bufs=1))
         relay = ctx.enter_context(tc.tile_pool(name="relay", bufs=1))
         acc = ctx.enter_context(tc.psum_pool(name="acc", bufs=PAGES))
         turn = ctx.enter_context(tc.psum_pool(name="turn", bufs=PAGES))
@@ -61,8 +58,8 @@ def tile_attend_pkv8_gate_kernel(tc, qT, k_words, k_scales, v_words, v_scales, v
         nc.vector.memset(k_scale_pool[:], 0)
         nc.vector.memset(vs_pool[0:VS_ROW, :], 0.0)
         k_scale_rows = k_scales[0].bitcast(I32)
-        for j in range(4):
-            nc.sync.dma_start(k_scale_pool[j:P:QUADRANT, :], k_scale_rows[j:16:4, :])
+        for j in range(RUN):
+            nc.sync.dma_start(k_scale_pool[j:P:QUADRANT, :], k_scale_rows[j:SCALE_ROWS:RUN, :])
         k_word_pool = held.tile([P, T], I32, name="k_word_pool")
         nc.sync.dma_start(k_word_pool[:], k_words[0].rearrange("g t r -> g (t r)").bitcast(I32))
         nc.sync.dma_start(q_raw[1][:], qT[1].rearrange("(g r) q -> g r q", r=PACK))
@@ -87,33 +84,28 @@ def tile_attend_pkv8_gate_kernel(tc, qT, k_words, k_scales, v_words, v_scales, v
         v_scale_pool = reused.tile([P, POOL_PAGES * DV // 4], I32, name="v_scale_pool", tag="q_raw0")
         nc.gpsimd.memset(v_scale_pool[:], 0)
         v_scale_rows = v_scales.rearrange("u f e -> f u e").bitcast(I32)
-        for j in range(4):
+        for j in range(RUN):
             nc.sync.dma_start(
                 v_scale_pool[V_SCALE_ROW + j : P : QUADRANT, :].rearrange("f (u e) -> f u e", u=POOL_PAGES),
-                v_scale_rows[j:16:4, :, :],
+                v_scale_rows[j:SCALE_ROWS:RUN, :, :],
             )
         v_word_pool = held.tile([P, POOL_PAGES * DV], I32, name="v_word_pool")
         nc.sync.dma_start(
             v_word_pool[:].rearrange("g (u e) -> g u e", u=POOL_PAGES),
             v_words.rearrange("u g e r -> g u (e r)").bitcast(I32),
         )
+
         vs_turned = [reused.tile([P, PACK], F32, name=f"vs_turned{page}", tag=f"vs_turned{page}", align_bytes=64) for page in range(PAGES)]
-
-        def turn_vs(page, slots):
-            nc.sync.dma_start(vs_turned[page][:], slots[VS_ROW : VS_ROW + 1, :].rearrange("o (g r) -> o g r", r=PACK))
-
         for page in range(PAGES):
-            turn_vs(page, vs_slots[:, page * PAGE : (page + 1) * PAGE])
+            row = vs_slots[VS_ROW : VS_ROW + 1, page * PAGE : (page + 1) * PAGE]
+            nc.sync.dma_start(vs_turned[page][:], row.rearrange("o (g r) -> o g r", r=PACK))
 
         half_tanh = held.tile([P, B * DV], F32, name="half_tanh")
         nc.scalar.activation(half_tanh[:], og_sb[:].rearrange("q b e -> q (b e)"), ACT.Tanh, scale=0.5)
         gate = held.tile([P, B * DV], F32, name="gate")
         nc.scalar.activation(gate[:], half_tanh[:], ACT.Copy, bias=0.5, scale=0.5)
 
-        neg_scores = [
-            late.tile([P, PACK, P], F32, name="neg_scores0", offset=NEG_SCORES1_AT, align_bytes=64),
-            held.tile([P, PACK, P], F32, name="neg_scores1", align_bytes=64),
-        ]
+        neg_scores = [held.tile([P, PACK, P], F32, name=f"neg_scores{b}", align_bytes=64) for b in range(B)]
         first_neg_max = [held.tile([P, 1], F32, name=f"first_neg_max{b}") for b in range(B)]
         neg_max = [held.tile([P, 1], F32, name=f"neg_max{b}") for b in range(B)]
         page_sums = [held.tile([P, SEQ_PAGES], F32, name=f"page_sums{b}") for b in range(B)]
@@ -176,11 +168,11 @@ def tile_attend_pkv8_gate_kernel(tc, qT, k_words, k_scales, v_words, v_scales, v
         score(LAST)
         row_max(1)
         exponentials(0)
-        row_max(2)
+        row_max(SEQ_PAGES)
         row_max(LAST)
         exponentials(1)
 
-        v_scale_slots = late.tile([P, PAGES * DV], U8, name="v_scale_slots", offset=V_SCALE_SLOTS_AT, align_bytes=64)
+        v_scale_slots = held.tile([P, PAGES * DV], U8, name="v_scale_slots", align_bytes=64)
         nc.vector.tensor_copy(v_scale_slots[:], v_scale_pool[:].bitcast(U8).indirect(column_list[:]))
         v_word_slots = {}
 
@@ -189,7 +181,7 @@ def tile_attend_pkv8_gate_kernel(tc, qT, k_words, k_scales, v_words, v_scales, v
             for e in range(count):
                 v_word_slots[first + e] = slots[:, e * DV : (e + 1) * DV]
 
-        gather_values(late.tile([P, SEQ_PAGES * DV], U32, name="v_word_slots1", offset=V_WORD_SLOTS_AT, align_bytes=64), SEQ_PAGES, SEQ_PAGES)
+        gather_values(held.tile([P, SEQ_PAGES * DV], U32, name="v_word_slots1", align_bytes=64), SEQ_PAGES, SEQ_PAGES)
 
         def weigh_on_scalar(page):
             planes = reused.tile([P, PACK, NQ], BF16, name=f"planes{page}", tag=f"planes{page}", align_bytes=64)
@@ -248,18 +240,18 @@ def tile_attend_pkv8_gate_kernel(tc, qT, k_words, k_scales, v_words, v_scales, v
         totals = reused.tile([P, B], F32, name="totals", tag="planes0", align_bytes=64)
         for b in range(B):
             nc.scalar.activation(totals[:, b : b + 1], page_sums[b][:, 0:1], ACT.Identity, bias=page_sums[b][:, 1:2], scale=1.0)
-        weigh_on_vector(2)
-        weigh_on_vector(3)
-        for page in (2, 3):
+        weigh_on_vector(SEQ_PAGES)
+        weigh_on_vector(LAST)
+        for page in (SEQ_PAGES, LAST):
             quantise(page)
             multiply(page)
         quantise(0)
-        gather_values(reused.tile([P, DV], U32, name="v_word_slots_page0", tag="vs_turned3", align_bytes=64), 0, 1)
+        gather_values(reused.tile([P, DV], U32, name="v_word_slots_page0", tag=f"vs_turned{LAST}", align_bytes=64), 0, 1)
         multiply(0)
-        gather_values(reused.tile([P, DV], U32, name="v_word_slots_page1", tag="w_bf2", align_bytes=64), 1, 1)
+        gather_values(reused.tile([P, DV], U32, name="v_word_slots_page1", tag=f"w_bf{SEQ_PAGES}", align_bytes=64), 1, 1)
         quantise(1)
         multiply(1)
-        inverses = reused.tile([P, B], F32, name="inverses", tag="vs_turned2", align_bytes=64)
+        inverses = reused.tile([P, B], F32, name="inverses", tag=f"vs_turned{SEQ_PAGES}", align_bytes=64)
         nc.vector.reciprocal(inverses[:], totals[:])
         finish(1)
         finish(0)

@@ -47,12 +47,12 @@ def tile_attend_pkv8_gate_kernel(tc, qT, k_words, k_scales, v_words, v_scales, v
         def entries(index_list, first, count):
             return index_list[:, first // GROUP : (first + count) // GROUP]
 
-        vs_pool = held.tile([P, T], F32, name="vs_pool")
-        nc.sync.dma_start(vs_pool[VS_ROW : VS_ROW + 1, :], vs[0:1, :])
         slot_list = held.tile([P, B * N // GROUP], U16, name="slot_list")
         nc.sync.dma_start(slot_list[:], offs)
         q_raw = [reused.tile([P, PACK, NQ], F32, name=f"q_raw{b}", tag=f"q_raw{b}") for b in range(B)]
         nc.sync.dma_start(q_raw[0][:], qT[0].rearrange("(g r) q -> g r q", r=PACK))
+        vs_pool = held.tile([P, T], F32, name="vs_pool")
+        nc.sync.dma_start(vs_pool[VS_ROW : VS_ROW + 1, :], vs[0:1, :])
 
         k_scale_pool = held.tile([P, T // 4], I32, name="k_scale_pool")
         nc.vector.memset(k_scale_pool[:], 0)
@@ -68,9 +68,6 @@ def tile_attend_pkv8_gate_kernel(tc, qT, k_words, k_scales, v_words, v_scales, v
         column_list = held.tile([P, PAGES * DV // GROUP], U16, name="column_list")
         nc.sync.dma_start(column_list[:], voffs)
 
-        vs_slots = held.tile([P, PAGES * PAGE], F32, name="vs_slots")
-        nc.vector.tensor_copy(vs_slots[:], vs_pool[:].indirect(slot_list[:]))
-
         q_bf = [held.tile([P, NQ, PACK], BF16, name=f"q_bf{b}", align_bytes=64) for b in range(B)]
         q_codes = [held.tile([P, NQ], U32, name=f"q_codes{b}", align_bytes=64) for b in range(B)]
         q_scales = [held.tile([P, NQ], U8, name=f"q_scales{b}", align_bytes=64) for b in range(B)]
@@ -78,6 +75,8 @@ def tile_attend_pkv8_gate_kernel(tc, qT, k_words, k_scales, v_words, v_scales, v
             nc.scalar.activation(q_bf[b][:], q_raw[b][:].rearrange("g r q -> g q r"), ACT.Copy)
             nc.vector.quantize_mx(out=q_codes[b][:].bitcast(FP8X4), scales=q_scales[b][:], in_=q_bf[b][:].rearrange("g q r -> g (q r)"))
 
+        vs_slots = held.tile([P, PAGES * PAGE], F32, name="vs_slots")
+        nc.scalar.activation(vs_slots[:], vs_pool[:].indirect(slot_list[:]), ACT.Copy)
         k_scale_slots = held.tile([P, B * N], U8, name="k_scale_slots", align_bytes=64)
         nc.vector.tensor_copy(k_scale_slots[:], k_scale_pool[:].bitcast(U8).indirect(slot_list[:]))
 

@@ -18,10 +18,6 @@ SCALE_ROWS = PAGE // 32
 VS_ROW = P - 1
 V_SCALE_ROW = 4
 
-IDENT_AT = 0
-LAST_KEYS_AT = IDENT_AT + P * 4
-FIRST_KEYS_AT = LAST_KEYS_AT - 64
-
 FLOPS = 2 * B * NQ * N * (D + DV)
 
 F32 = mybir.dt.float32
@@ -40,7 +36,6 @@ def tile_attend_pkv8_gate_kernel(tc, qT, k_words, k_scales, v_words, v_scales, v
     with ExitStack() as ctx:
         held = ctx.enter_context(tc.tile_pool(name="held", bufs=1))
         reused = ctx.enter_context(tc.tile_pool(name="reused", bufs=1))
-        relay = ctx.enter_context(tc.tile_pool(name="relay", bufs=1))
         acc = ctx.enter_context(tc.psum_pool(name="acc", bufs=PAGES))
         turn = ctx.enter_context(tc.psum_pool(name="turn", bufs=PAGES))
 
@@ -49,24 +44,25 @@ def tile_attend_pkv8_gate_kernel(tc, qT, k_words, k_scales, v_words, v_scales, v
 
         slot_list = held.tile([P, B * N // GROUP], U16, name="slot_list")
         nc.sync.dma_start(slot_list[:], offs)
-        q_raw = [reused.tile([P, PACK, NQ], F32, name=f"q_raw{b}", tag=f"q_raw{b}") for b in range(B)]
+        q_raw = [reused.tile([P, PACK, NQ], F32, name=f"q_raw{b}", tag=f"q_raw{b}", align_bytes=256) for b in range(B)]
         nc.sync.dma_start(q_raw[0][:], qT[0].rearrange("(g r) q -> g r q", r=PACK))
-        vs_pool = held.tile([P, T], F32, name="vs_pool")
-        nc.sync.dma_start(vs_pool[VS_ROW : VS_ROW + 1, :], vs[0:1, :])
+        vs_pool = held.tile([P, T], F32, name="vs_pool", align_bytes=256)
+        column_list = held.tile([P, PAGES * DV // GROUP], U16, name="column_list")
+        nc.sync.dma_start(column_list[:], voffs)
 
-        k_scale_pool = held.tile([P, T // 4], I32, name="k_scale_pool")
+        k_scale_pool = held.tile([P, T // 4], I32, name="k_scale_pool", align_bytes=256)
         nc.vector.memset(k_scale_pool[:], 0)
         nc.vector.memset(vs_pool[0:VS_ROW, :], 0.0)
         k_scale_rows = k_scales[0].bitcast(I32)
         for j in range(RUN):
             nc.sync.dma_start(k_scale_pool[j:P:QUADRANT, :], k_scale_rows[j:SCALE_ROWS:RUN, :])
-        k_word_pool = held.tile([P, T], I32, name="k_word_pool")
+            if j == 0:
+                nc.sync.dma_start(vs_pool[VS_ROW : VS_ROW + 1, :], vs[0:1, :])
+        k_word_pool = held.tile([P, T], I32, name="k_word_pool", align_bytes=256)
         nc.sync.dma_start(k_word_pool[:], k_words[0].rearrange("g t r -> g (t r)").bitcast(I32))
         nc.sync.dma_start(q_raw[1][:], qT[1].rearrange("(g r) q -> g r q", r=PACK))
-        og_sb = held.tile([P, B, DV], F32, name="og_sb")
+        og_sb = held.tile([P, B, DV], F32, name="og_sb", align_bytes=256)
         nc.sync.dma_start(og_sb[:], og.rearrange("b q e -> q b e"))
-        column_list = held.tile([P, PAGES * DV // GROUP], U16, name="column_list")
-        nc.sync.dma_start(column_list[:], voffs)
 
         q_bf = [held.tile([P, NQ, PACK], BF16, name=f"q_bf{b}", align_bytes=64) for b in range(B)]
         q_codes = [held.tile([P, NQ], U32, name=f"q_codes{b}", align_bytes=64) for b in range(B)]
@@ -80,7 +76,7 @@ def tile_attend_pkv8_gate_kernel(tc, qT, k_words, k_scales, v_words, v_scales, v
         k_scale_slots = held.tile([P, B * N], U8, name="k_scale_slots", align_bytes=64)
         nc.vector.tensor_copy(k_scale_slots[:], k_scale_pool[:].bitcast(U8).indirect(slot_list[:]))
 
-        v_scale_pool = reused.tile([P, POOL_PAGES * DV // 4], I32, name="v_scale_pool", tag="q_raw0")
+        v_scale_pool = reused.tile([P, POOL_PAGES * DV // 4], I32, name="v_scale_pool", tag="q_raw0", align_bytes=256)
         nc.gpsimd.memset(v_scale_pool[:], 0)
         v_scale_rows = v_scales.rearrange("u f e -> f u e").bitcast(I32)
         for j in range(RUN):
@@ -88,7 +84,7 @@ def tile_attend_pkv8_gate_kernel(tc, qT, k_words, k_scales, v_words, v_scales, v
                 v_scale_pool[V_SCALE_ROW + j : P : QUADRANT, :].rearrange("f (u e) -> f u e", u=POOL_PAGES),
                 v_scale_rows[j:SCALE_ROWS:RUN, :, :],
             )
-        v_word_pool = held.tile([P, POOL_PAGES * DV], I32, name="v_word_pool")
+        v_word_pool = held.tile([P, POOL_PAGES * DV], I32, name="v_word_pool", align_bytes=256)
         nc.sync.dma_start(
             v_word_pool[:].rearrange("g (u e) -> g u e", u=POOL_PAGES),
             v_words.rearrange("u g e r -> g u (e r)").bitcast(I32),
@@ -118,10 +114,7 @@ def tile_attend_pkv8_gate_kernel(tc, qT, k_words, k_scales, v_words, v_scales, v
 
         def score(page):
             b = page // SEQ_PAGES
-            if page in (0, LAST):
-                keys = relay.tile([P, PAGE], U32, name=f"k_word_slots{page}", offset=LAST_KEYS_AT if page else FIRST_KEYS_AT, align_bytes=64)
-            else:
-                keys = held.tile([P, PAGE], U32, name=f"k_word_slots{page}", align_bytes=64)
+            keys = reused.tile([P, PAGE], U32, name=f"k_word_slots{page}", tag=f"keys{page % LAST}", align_bytes=64)
             nc.vector.tensor_copy(keys[:], k_word_pool[:].bitcast(U32).indirect(entries(slot_list, page * PAGE, PAGE)))
             scores[page] = acc.tile([P, PAGE], F32, name="score", tag="acc")
             nc.tensor.matmul_mx(
@@ -161,7 +154,7 @@ def tile_attend_pkv8_gate_kernel(tc, qT, k_words, k_scales, v_words, v_scales, v
 
         for page in range(LAST):
             score(page)
-        ident = relay.tile([P, P], F32, name="ident", offset=IDENT_AT, align_bytes=64)
+        ident = reused.tile([P, P], F32, name="ident", tag="keys2", align_bytes=64)
         make_identity(nc, ident[:])
         row_max(0)
         score(LAST)

@@ -16,7 +16,17 @@ QUADRANT = 32
 RUN = 4
 SCALE_ROWS = PAGE // 32
 VS_ROW = P - 1
-V_SCALE_ROW = 4
+SPREAD = P // SCALE_ROWS
+
+STEP = 256
+LAST_KEYS_AT = 0
+Q_RAW1_AT = LAST_KEYS_AT + PAGE * 4 - STEP
+OG_AT = Q_RAW1_AT + PACK * NQ * 4
+SPREAD1_AT = OG_AT + B * DV * 4
+Q_BF0_AT = OG_AT - STEP
+Q_BF0_BYTES = SPREAD1_AT + STEP - Q_BF0_AT
+V_WORDS_AT = SPREAD1_AT + N - STEP
+Q_RAW0_AT = V_WORDS_AT + POOL_PAGES * DV * 4
 
 FLOPS = 2 * B * NQ * N * (D + DV)
 
@@ -36,6 +46,7 @@ def tile_attend_pkv8_gate_kernel(tc, qT, k_words, k_scales, v_words, v_scales, v
     with ExitStack() as ctx:
         held = ctx.enter_context(tc.tile_pool(name="held", bufs=1))
         reused = ctx.enter_context(tc.tile_pool(name="reused", bufs=1))
+        placed = ctx.enter_context(tc.tile_pool(name="placed", bufs=1))
         acc = ctx.enter_context(tc.psum_pool(name="acc", bufs=PAGES))
         turn = ctx.enter_context(tc.psum_pool(name="turn", bufs=PAGES))
 
@@ -44,63 +55,74 @@ def tile_attend_pkv8_gate_kernel(tc, qT, k_words, k_scales, v_words, v_scales, v
 
         slot_list = held.tile([P, B * N // GROUP], U16, name="slot_list")
         nc.sync.dma_start(slot_list[:], offs)
-        q_raw = [reused.tile([P, PACK, NQ], F32, name=f"q_raw{b}", tag=f"q_raw{b}", align_bytes=256) for b in range(B)]
-        nc.sync.dma_start(q_raw[0][:], qT[0].rearrange("(g r) q -> g r q", r=PACK))
+        q_raw0 = placed.tile([P, PACK, NQ], F32, name="q_raw0", offset=Q_RAW0_AT, align_bytes=256)
+        nc.sync.dma_start(q_raw0[:], qT[0].rearrange("(g r) q -> g r q", r=PACK))
         vs_pool = held.tile([P, T], F32, name="vs_pool", align_bytes=256)
         column_list = held.tile([P, PAGES * DV // GROUP], U16, name="column_list")
         nc.sync.dma_start(column_list[:], voffs)
 
-        k_scale_pool = held.tile([P, T // 4], I32, name="k_scale_pool", align_bytes=256)
+        k_scale_pool = reused.tile([P, T // 4], I32, name="k_scale_pool", tag="k_scale_pool", align_bytes=256)
         nc.vector.memset(k_scale_pool[:], 0)
         nc.vector.memset(vs_pool[0:VS_ROW, :], 0.0)
-        k_scale_rows = k_scales[0].bitcast(I32)
-        for j in range(RUN):
-            nc.sync.dma_start(k_scale_pool[j:P:QUADRANT, :], k_scale_rows[j:SCALE_ROWS:RUN, :])
-            if j == 0:
-                nc.sync.dma_start(vs_pool[VS_ROW : VS_ROW + 1, :], vs[0:1, :])
+        nc.sync.dma_start(k_scale_pool[0:P:SPREAD, :], k_scales[0].bitcast(I32))
+        nc.sync.dma_start(vs_pool[VS_ROW : VS_ROW + 1, :], vs[0:1, :])
         k_word_pool = held.tile([P, T], I32, name="k_word_pool", align_bytes=256)
         nc.sync.dma_start(k_word_pool[:], k_words[0].rearrange("g t r -> g (t r)").bitcast(I32))
-        nc.sync.dma_start(q_raw[1][:], qT[1].rearrange("(g r) q -> g r q", r=PACK))
-        og_sb = held.tile([P, B, DV], F32, name="og_sb", align_bytes=256)
-        nc.sync.dma_start(og_sb[:], og.rearrange("b q e -> q b e"))
 
-        q_bf = [held.tile([P, NQ, PACK], BF16, name=f"q_bf{b}", align_bytes=64) for b in range(B)]
-        q_codes = [held.tile([P, NQ], U32, name=f"q_codes{b}", align_bytes=64) for b in range(B)]
-        q_scales = [held.tile([P, NQ], U8, name=f"q_scales{b}", align_bytes=64) for b in range(B)]
+        q_bf = [
+            placed.tile([P, Q_BF0_BYTES // (2 * PACK), PACK], BF16, name="q_bf0", offset=Q_BF0_AT, align_bytes=256),
+            reused.tile([P, NQ, PACK], BF16, name="q_bf1", tag="q_bf1", align_bytes=64),
+        ]
+        q_codes = [reused.tile([P, NQ], U32, name=f"q_codes{b}", tag=f"q_codes{b}", align_bytes=64) for b in range(B)]
+        q_scales = [reused.tile([P, NQ], U8, name=f"q_scales{b}", tag=f"q_scales{b}", align_bytes=64) for b in range(B)]
+
+        def cast(b, raw):
+            nc.scalar.activation(q_bf[b][:, 0:NQ, :], raw[:].rearrange("g r q -> g q r"), ACT.Copy)
+
+        def quantise_queries(b):
+            nc.vector.quantize_mx(out=q_codes[b][:].bitcast(FP8X4), scales=q_scales[b][:], in_=q_bf[b][:, 0:NQ, :].rearrange("g q r -> g (q r)"))
+
+        cast(0, q_raw0)
+        k_scale_slots = [placed.tile([P, N // 4], I32, name=f"k_scale_slots{b}", offset=Q_RAW0_AT + b * N, align_bytes=256) for b in range(B)]
         for b in range(B):
-            nc.scalar.activation(q_bf[b][:], q_raw[b][:].rearrange("g r q -> g q r"), ACT.Copy)
-            nc.vector.quantize_mx(out=q_codes[b][:].bitcast(FP8X4), scales=q_scales[b][:], in_=q_bf[b][:].rearrange("g q r -> g (q r)"))
+            nc.gpsimd.memset(k_scale_slots[b][:], 0)
+
+        def key_scales(b, spread):
+            nc.vector.tensor_copy(spread[:], k_scale_pool[:].bitcast(U8).indirect(entries(slot_list, b * N, N)))
+            for j in range(RUN):
+                nc.sync.dma_start(k_scale_slots[b][j:P:QUADRANT, :], spread[:].bitcast(I32)[j * SPREAD : P : QUADRANT, :])
 
         vs_slots = held.tile([P, PAGES * PAGE], F32, name="vs_slots")
         nc.scalar.activation(vs_slots[:], vs_pool[:].indirect(slot_list[:]), ACT.Copy)
-        k_scale_slots = held.tile([P, B * N], U8, name="k_scale_slots", align_bytes=64)
-        nc.vector.tensor_copy(k_scale_slots[:], k_scale_pool[:].bitcast(U8).indirect(slot_list[:]))
+        key_scales(0, held.tile([P, N], U8, name="k_scale_spread0", align_bytes=64))
+        quantise_queries(0)
+        q_raw1 = placed.tile([P, PACK, NQ], F32, name="q_raw1", offset=Q_RAW1_AT, align_bytes=256)
+        nc.sync.dma_start(q_raw1[:], qT[1].rearrange("(g r) q -> g r q", r=PACK))
+        og_sb = placed.tile([P, B, DV], F32, name="og_sb", offset=OG_AT, align_bytes=256)
+        nc.sync.dma_start(og_sb[:], og.rearrange("b q e -> q b e"))
+        key_scales(1, placed.tile([P, N], U8, name="k_scale_spread1", offset=SPREAD1_AT, align_bytes=256))
+        cast(1, q_raw1)
+        quantise_queries(1)
 
-        v_scale_pool = reused.tile([P, POOL_PAGES * DV // 4], I32, name="v_scale_pool", tag="q_raw0", align_bytes=256)
+        v_scale_pool = reused.tile([P, POOL_PAGES * DV // 4], I32, name="v_scale_pool", tag="k_scale_pool", align_bytes=256)
         nc.gpsimd.memset(v_scale_pool[:], 0)
         v_scale_rows = v_scales.rearrange("u f e -> f u e").bitcast(I32)
         for j in range(RUN):
             nc.sync.dma_start(
-                v_scale_pool[V_SCALE_ROW + j : P : QUADRANT, :].rearrange("f (u e) -> f u e", u=POOL_PAGES),
-                v_scale_rows[j:SCALE_ROWS:RUN, :, :],
+                v_scale_pool[j:P:QUADRANT, :].rearrange("f (u e) -> f u e", u=POOL_PAGES), v_scale_rows[j:SCALE_ROWS:RUN, :, :]
             )
-        v_word_pool = held.tile([P, POOL_PAGES * DV], I32, name="v_word_pool", align_bytes=256)
+        v_word_pool = placed.tile([P, POOL_PAGES * DV], I32, name="v_word_pool", offset=V_WORDS_AT, align_bytes=256)
         nc.sync.dma_start(
             v_word_pool[:].rearrange("g (u e) -> g u e", u=POOL_PAGES),
             v_words.rearrange("u g e r -> g u (e r)").bitcast(I32),
         )
-
-        vs_turned = [reused.tile([P, PACK], F32, name=f"vs_turned{page}", tag=f"vs_turned{page}", align_bytes=64) for page in range(PAGES)]
-        for page in range(PAGES):
-            row = vs_slots[VS_ROW : VS_ROW + 1, page * PAGE : (page + 1) * PAGE]
-            nc.sync.dma_start(vs_turned[page][:], row.rearrange("o (g r) -> o g r", r=PACK))
 
         half_tanh = held.tile([P, B * DV], F32, name="half_tanh")
         nc.scalar.activation(half_tanh[:], og_sb[:].rearrange("q b e -> q (b e)"), ACT.Tanh, scale=0.5)
         gate = held.tile([P, B * DV], F32, name="gate")
         nc.scalar.activation(gate[:], half_tanh[:], ACT.Copy, bias=0.5, scale=0.5)
 
-        neg_scores = [held.tile([P, PACK, P], F32, name=f"neg_scores{b}", align_bytes=64) for b in range(B)]
+        neg_scores = [reused.tile([P, PACK, P], F32, name=f"neg_scores{b}", tag=f"q_bf{b + 1}", align_bytes=64) for b in range(B)]
         first_neg_max = [held.tile([P, 1], F32, name=f"first_neg_max{b}") for b in range(B)]
         neg_max = [held.tile([P, 1], F32, name=f"neg_max{b}") for b in range(B)]
         page_sums = [held.tile([P, SEQ_PAGES], F32, name=f"page_sums{b}") for b in range(B)]
@@ -113,8 +135,11 @@ def tile_attend_pkv8_gate_kernel(tc, qT, k_words, k_scales, v_words, v_scales, v
         sums = {}
 
         def score(page):
-            b = page // SEQ_PAGES
-            keys = reused.tile([P, PAGE], U32, name=f"k_word_slots{page}", tag=f"keys{page % LAST}", align_bytes=64)
+            b, h = divmod(page, SEQ_PAGES)
+            if page == LAST:
+                keys = placed.tile([P, PAGE], U32, name="k_word_slots_last", offset=LAST_KEYS_AT, align_bytes=256)
+            else:
+                keys = reused.tile([P, PAGE], U32, name=f"k_word_slots{page}", tag=f"keys{page}", align_bytes=64)
             nc.vector.tensor_copy(keys[:], k_word_pool[:].bitcast(U32).indirect(entries(slot_list, page * PAGE, PAGE)))
             scores[page] = acc.tile([P, PAGE], F32, name="score", tag="acc")
             nc.tensor.matmul_mx(
@@ -122,7 +147,7 @@ def tile_attend_pkv8_gate_kernel(tc, qT, k_words, k_scales, v_words, v_scales, v
                 lhsT=q_codes[b][:].bitcast(FP8X4),
                 lhsT_scale=q_scales[b][:],
                 rhs=keys[:].bitcast(FP8X4),
-                rhs_scale=k_scale_slots[:, page * PAGE : (page + 1) * PAGE],
+                rhs_scale=k_scale_slots[b][:].bitcast(U8)[:, h * PAGE : (h + 1) * PAGE],
                 start=True,
                 stop=True,
             )
@@ -158,6 +183,11 @@ def tile_attend_pkv8_gate_kernel(tc, qT, k_words, k_scales, v_words, v_scales, v
         make_identity(nc, ident[:])
         row_max(0)
         score(LAST)
+        turned_tags = ("q_codes0", "q_scales0", "q_codes1", "q_scales1")
+        vs_turned = [reused.tile([P, PACK], F32, name=f"vs_turned{page}", tag=turned_tags[page], align_bytes=64) for page in range(PAGES)]
+        for page in range(PAGES):
+            row = vs_slots[VS_ROW : VS_ROW + 1, page * PAGE : (page + 1) * PAGE]
+            nc.sync.dma_start(vs_turned[page][:], row.rearrange("o (g r) -> o g r", r=PACK))
         row_max(1)
         exponentials(0)
         row_max(SEQ_PAGES)
@@ -208,7 +238,7 @@ def tile_attend_pkv8_gate_kernel(tc, qT, k_words, k_scales, v_words, v_scales, v
                     lhsT=w_codes[page][:].bitcast(FP8X4),
                     lhsT_scale=w_scales[page][:],
                     rhs=v_word_slots[page][:, part * width : (part + 1) * width].bitcast(FP8X4),
-                    rhs_scale=v_scale_slots[V_SCALE_ROW:P, at : at + width],
+                    rhs_scale=v_scale_slots[:, at : at + width],
                     start=h == 0,
                     stop=h == SEQ_PAGES - 1,
                 )
@@ -238,12 +268,12 @@ def tile_attend_pkv8_gate_kernel(tc, qT, k_words, k_scales, v_words, v_scales, v
             quantise(page)
             multiply(page)
         quantise(0)
-        gather_values(reused.tile([P, DV], U32, name="v_word_slots_page0", tag=f"vs_turned{LAST}", align_bytes=64), 0, 1)
+        gather_values(reused.tile([P, DV], U32, name="v_word_slots_page0", tag=turned_tags[LAST], align_bytes=64), 0, 1)
         multiply(0)
         gather_values(reused.tile([P, DV], U32, name="v_word_slots_page1", tag=f"w_bf{SEQ_PAGES}", align_bytes=64), 1, 1)
         quantise(1)
         multiply(1)
-        inverses = reused.tile([P, B], F32, name="inverses", tag=f"vs_turned{SEQ_PAGES}", align_bytes=64)
+        inverses = reused.tile([P, B], F32, name="inverses", tag=turned_tags[SEQ_PAGES], align_bytes=64)
         nc.vector.reciprocal(inverses[:], totals[:])
         finish(1)
         finish(0)

@@ -19,14 +19,13 @@ VS_ROW = P - 1
 SPREAD = P // SCALE_ROWS
 
 STEP = 256
-LAST_KEYS_AT = 0
-Q_RAW1_AT = LAST_KEYS_AT + PAGE * 4 - STEP
-OG_AT = Q_RAW1_AT + PACK * NQ * 4
+OG_AT = 0
 SPREAD1_AT = OG_AT + B * DV * 4
-Q_BF0_AT = OG_AT - STEP
-Q_BF0_BYTES = SPREAD1_AT + STEP - Q_BF0_AT
-V_WORDS_AT = SPREAD1_AT + N - STEP
-Q_RAW0_AT = V_WORDS_AT + POOL_PAGES * DV * 4
+LAST_KEYS_AT = SPREAD1_AT + N
+Q_RAW1_AT = LAST_KEYS_AT + PAGE * 4 - STEP
+V_WORDS_AT = Q_RAW1_AT + PACK * NQ * 4 - STEP
+Q_BF0_AT = SPREAD1_AT - STEP
+Q_BF0_BYTES = Q_RAW1_AT + STEP - Q_BF0_AT
 
 FLOPS = 2 * B * NQ * N * (D + DV)
 
@@ -55,7 +54,7 @@ def tile_attend_pkv8_gate_kernel(tc, qT, k_words, k_scales, v_words, v_scales, v
 
         slot_list = held.tile([P, B * N // GROUP], U16, name="slot_list")
         nc.sync.dma_start(slot_list[:], offs)
-        q_raw0 = placed.tile([P, PACK, NQ], F32, name="q_raw0", offset=Q_RAW0_AT, align_bytes=256)
+        q_raw0 = held.tile([P, PACK, NQ], F32, name="q_raw0", align_bytes=256)
         nc.sync.dma_start(q_raw0[:], qT[0].rearrange("(g r) q -> g r q", r=PACK))
         vs_pool = held.tile([P, T], F32, name="vs_pool", align_bytes=256)
         column_list = held.tile([P, PAGES * DV // GROUP], U16, name="column_list")
@@ -83,9 +82,9 @@ def tile_attend_pkv8_gate_kernel(tc, qT, k_words, k_scales, v_words, v_scales, v
             nc.vector.quantize_mx(out=q_codes[b][:].bitcast(FP8X4), scales=q_scales[b][:], in_=q_bf[b][:, 0:NQ, :].rearrange("g q r -> g (q r)"))
 
         cast(0, q_raw0)
-        k_scale_slots = [placed.tile([P, N // 4], I32, name=f"k_scale_slots{b}", offset=Q_RAW0_AT + b * N, align_bytes=256) for b in range(B)]
+        k_scale_slots = [held.tile([P, N // 4], I32, name=f"k_scale_slots{b}", align_bytes=256) for b in range(B)]
         for b in range(B):
-            nc.gpsimd.memset(k_scale_slots[b][:], 0)
+            nc.vector.memset(k_scale_slots[b][:], 0)
 
         def key_scales(b, spread):
             nc.vector.tensor_copy(spread[:], k_scale_pool[:].bitcast(U8).indirect(entries(slot_list, b * N, N)))
@@ -105,7 +104,7 @@ def tile_attend_pkv8_gate_kernel(tc, qT, k_words, k_scales, v_words, v_scales, v
         quantise_queries(1)
 
         v_scale_pool = reused.tile([P, POOL_PAGES * DV // 4], I32, name="v_scale_pool", tag="k_scale_pool", align_bytes=256)
-        nc.gpsimd.memset(v_scale_pool[:], 0)
+        nc.vector.memset(v_scale_pool[:], 0)
         v_scale_rows = v_scales.rearrange("u f e -> f u e").bitcast(I32)
         for j in range(RUN):
             nc.sync.dma_start(

@@ -19,13 +19,10 @@ VS_ROW = P - 1
 SPREAD = P // SCALE_ROWS
 
 STEP = 256
-OG_AT = 0
-SPREAD1_AT = OG_AT + B * DV * 4
-LAST_KEYS_AT = SPREAD1_AT + N
-Q_RAW1_AT = LAST_KEYS_AT + PAGE * 4 - STEP
-V_WORDS_AT = Q_RAW1_AT + PACK * NQ * 4 - STEP
-Q_BF0_AT = SPREAD1_AT - STEP
-Q_BF0_BYTES = Q_RAW1_AT + STEP - Q_BF0_AT
+Q_RAW1_AT = 0
+V_SCALES_AT = Q_RAW1_AT + PACK * NQ * 4
+K_SCALES_AT = V_SCALES_AT - STEP
+OG_AT = K_SCALES_AT + T - STEP
 
 FLOPS = 2 * B * NQ * N * (D + DV)
 
@@ -60,7 +57,7 @@ def tile_attend_pkv8_gate_kernel(tc, qT, k_words, k_scales, v_words, v_scales, v
         column_list = held.tile([P, PAGES * DV // GROUP], U16, name="column_list")
         nc.sync.dma_start(column_list[:], voffs)
 
-        k_scale_pool = reused.tile([P, T // 4], I32, name="k_scale_pool", tag="k_scale_pool", align_bytes=256)
+        k_scale_pool = placed.tile([P, T // 4], I32, name="k_scale_pool", offset=K_SCALES_AT, align_bytes=256)
         nc.vector.memset(k_scale_pool[:], 0)
         nc.vector.memset(vs_pool[0:VS_ROW, :], 0.0)
         nc.sync.dma_start(k_scale_pool[0:P:SPREAD, :], k_scales[0].bitcast(I32))
@@ -68,49 +65,42 @@ def tile_attend_pkv8_gate_kernel(tc, qT, k_words, k_scales, v_words, v_scales, v
         k_word_pool = held.tile([P, T], I32, name="k_word_pool", align_bytes=256)
         nc.sync.dma_start(k_word_pool[:], k_words[0].rearrange("g t r -> g (t r)").bitcast(I32))
 
-        q_bf = [
-            placed.tile([P, Q_BF0_BYTES // (2 * PACK), PACK], BF16, name="q_bf0", offset=Q_BF0_AT, align_bytes=256),
-            reused.tile([P, NQ, PACK], BF16, name="q_bf1", tag="q_bf1", align_bytes=64),
-        ]
+        q_bf = [reused.tile([P, NQ, PACK], BF16, name=f"q_bf{b}", tag=f"q_bf{b}", align_bytes=256) for b in range(B)]
         q_codes = [reused.tile([P, NQ], U32, name=f"q_codes{b}", tag=f"q_codes{b}", align_bytes=64) for b in range(B)]
         q_scales = [reused.tile([P, NQ], U8, name=f"q_scales{b}", tag=f"q_scales{b}", align_bytes=64) for b in range(B)]
 
         def cast(b, raw):
-            nc.scalar.activation(q_bf[b][:, 0:NQ, :], raw[:].rearrange("g r q -> g q r"), ACT.Copy)
+            nc.scalar.activation(q_bf[b][:], raw[:].rearrange("g r q -> g q r"), ACT.Copy)
 
         def quantise_queries(b):
-            nc.vector.quantize_mx(out=q_codes[b][:].bitcast(FP8X4), scales=q_scales[b][:], in_=q_bf[b][:, 0:NQ, :].rearrange("g q r -> g (q r)"))
+            nc.vector.quantize_mx(out=q_codes[b][:].bitcast(FP8X4), scales=q_scales[b][:], in_=q_bf[b][:].rearrange("g q r -> g (q r)"))
 
         cast(0, q_raw0)
-        k_scale_slots = [held.tile([P, N // 4], I32, name=f"k_scale_slots{b}", align_bytes=256) for b in range(B)]
-        for b in range(B):
-            nc.vector.memset(k_scale_slots[b][:], 0)
-
-        def key_scales(b, spread):
-            nc.vector.tensor_copy(spread[:], k_scale_pool[:].bitcast(U8).indirect(entries(slot_list, b * N, N)))
-            for j in range(RUN):
-                nc.sync.dma_start(k_scale_slots[b][j:P:QUADRANT, :], spread[:].bitcast(I32)[j * SPREAD : P : QUADRANT, :])
+        k_scale_slots = held.tile([P, B * N // 4], I32, name="k_scale_slots", align_bytes=256)
+        nc.vector.memset(k_scale_slots[:], 0)
 
         vs_slots = held.tile([P, PAGES * PAGE], F32, name="vs_slots")
         nc.scalar.activation(vs_slots[:], vs_pool[:].indirect(slot_list[:]), ACT.Copy)
-        key_scales(0, held.tile([P, N], U8, name="k_scale_spread0", align_bytes=64))
-        quantise_queries(0)
+        spread = held.tile([P, B * N], U8, name="k_scale_spread", align_bytes=64)
+        nc.vector.tensor_copy(spread[:], k_scale_pool[:].bitcast(U8).indirect(slot_list[:]))
+        for j in range(RUN):
+            nc.sync.dma_start(k_scale_slots[j:P:QUADRANT, :], spread[:].bitcast(I32)[j * SPREAD : P : QUADRANT, :])
         q_raw1 = placed.tile([P, PACK, NQ], F32, name="q_raw1", offset=Q_RAW1_AT, align_bytes=256)
         nc.sync.dma_start(q_raw1[:], qT[1].rearrange("(g r) q -> g r q", r=PACK))
         og_sb = placed.tile([P, B, DV], F32, name="og_sb", offset=OG_AT, align_bytes=256)
         nc.sync.dma_start(og_sb[:], og.rearrange("b q e -> q b e"))
-        key_scales(1, placed.tile([P, N], U8, name="k_scale_spread1", offset=SPREAD1_AT, align_bytes=256))
+        v_scale_pool = placed.tile([P, POOL_PAGES * DV // 4], I32, name="v_scale_pool", offset=V_SCALES_AT, align_bytes=256)
+        nc.vector.memset(v_scale_pool[:], 0)
+        quantise_queries(0)
         cast(1, q_raw1)
         quantise_queries(1)
 
-        v_scale_pool = reused.tile([P, POOL_PAGES * DV // 4], I32, name="v_scale_pool", tag="k_scale_pool", align_bytes=256)
-        nc.vector.memset(v_scale_pool[:], 0)
         v_scale_rows = v_scales.rearrange("u f e -> f u e").bitcast(I32)
         for j in range(RUN):
             nc.sync.dma_start(
                 v_scale_pool[j:P:QUADRANT, :].rearrange("f (u e) -> f u e", u=POOL_PAGES), v_scale_rows[j:SCALE_ROWS:RUN, :, :]
             )
-        v_word_pool = placed.tile([P, POOL_PAGES * DV], I32, name="v_word_pool", offset=V_WORDS_AT, align_bytes=256)
+        v_word_pool = reused.tile([P, POOL_PAGES * DV], I32, name="v_word_pool", tag="q_bf0", align_bytes=256)
         nc.sync.dma_start(
             v_word_pool[:].rearrange("g (u e) -> g u e", u=POOL_PAGES),
             v_words.rearrange("u g e r -> g u (e r)").bitcast(I32),
@@ -121,7 +111,7 @@ def tile_attend_pkv8_gate_kernel(tc, qT, k_words, k_scales, v_words, v_scales, v
         gate = held.tile([P, B * DV], F32, name="gate")
         nc.scalar.activation(gate[:], half_tanh[:], ACT.Copy, bias=0.5, scale=0.5)
 
-        neg_scores = [reused.tile([P, PACK, P], F32, name=f"neg_scores{b}", tag=f"q_bf{b + 1}", align_bytes=64) for b in range(B)]
+        neg_scores = [reused.tile([P, PACK, P], F32, name=f"neg_scores{b}", tag=f"q_bf{b + 1}", align_bytes=256) for b in range(B)]
         first_neg_max = [held.tile([P, 1], F32, name=f"first_neg_max{b}") for b in range(B)]
         neg_max = [held.tile([P, 1], F32, name=f"neg_max{b}") for b in range(B)]
         page_sums = [held.tile([P, SEQ_PAGES], F32, name=f"page_sums{b}") for b in range(B)]
@@ -134,9 +124,9 @@ def tile_attend_pkv8_gate_kernel(tc, qT, k_words, k_scales, v_words, v_scales, v
         sums = {}
 
         def score(page):
-            b, h = divmod(page, SEQ_PAGES)
+            b = page // SEQ_PAGES
             if page == LAST:
-                keys = placed.tile([P, PAGE], U32, name="k_word_slots_last", offset=LAST_KEYS_AT, align_bytes=256)
+                keys = placed.tile([P, PAGE], U32, name="k_word_slots_last", offset=Q_RAW1_AT, align_bytes=256)
             else:
                 keys = reused.tile([P, PAGE], U32, name=f"k_word_slots{page}", tag=f"keys{page}", align_bytes=64)
             nc.vector.tensor_copy(keys[:], k_word_pool[:].bitcast(U32).indirect(entries(slot_list, page * PAGE, PAGE)))
@@ -146,7 +136,7 @@ def tile_attend_pkv8_gate_kernel(tc, qT, k_words, k_scales, v_words, v_scales, v
                 lhsT=q_codes[b][:].bitcast(FP8X4),
                 lhsT_scale=q_scales[b][:],
                 rhs=keys[:].bitcast(FP8X4),
-                rhs_scale=k_scale_slots[b][:].bitcast(U8)[:, h * PAGE : (h + 1) * PAGE],
+                rhs_scale=k_scale_slots[:].bitcast(U8)[:, page * PAGE : (page + 1) * PAGE],
                 start=True,
                 stop=True,
             )

from contextlib import ExitStack

import concourse.mybir as mybir
from concourse.masks import make_identity

B, N, T, D, DV, NQ = 2, 1024, 4096, 512, 256, 128
P = 128
PACK = 4
PAGE = P * PACK
SEQ_PAGES = N // PAGE
PAGES = B * SEQ_PAGES
LAST = PAGES - 1
POOL_PAGES = T // PAGE
GROUP = 16
QUADRANT = 32
RUN = 4
SCALE_ROWS = PAGE // 32
VS_ROW = P - 1
SPREAD = P // SCALE_ROWS

STEP = 256
Q_RAW1_AT = 0
V_SCALES_AT = Q_RAW1_AT + PACK * NQ * 4
K_SCALES_AT = V_SCALES_AT - STEP
OG_AT = K_SCALES_AT + T - STEP

FLOPS = 2 * B * NQ * N * (D + DV)

F32 = mybir.dt.float32
BF16 = mybir.dt.bfloat16
I32 = mybir.dt.int32
U32 = mybir.dt.uint32
U16 = mybir.dt.uint16
U8 = mybir.dt.uint8
FP8X4 = mybir.dt.float8_e4m3fn_x4
ALU = mybir.AluOpType
ACT = mybir.ActivationFunctionType


def tile_attend_pkv8_gate_kernel(tc, qT, k_words, k_scales, v_words, v_scales, vs, og, offs, voffs, out):
    nc = tc.nc
    with ExitStack() as ctx:
        held = ctx.enter_context(tc.tile_pool(name="held", bufs=1))
        reused = ctx.enter_context(tc.tile_pool(name="reused", bufs=1))
        placed = ctx.enter_context(tc.tile_pool(name="placed", bufs=1))
        acc = ctx.enter_context(tc.psum_pool(name="acc", bufs=PAGES))
        turn = ctx.enter_context(tc.psum_pool(name="turn", bufs=PAGES))

        def entries(index_list, first, count):
            return index_list[:, first // GROUP : (first + count) // GROUP]

        slot_list = held.tile([P, B * N // GROUP], U16, name="slot_list")
        nc.sync.dma_start(slot_list[:], offs)
        q_raw0 = held.tile([P, PACK, NQ], F32, name="q_raw0", align_bytes=256)
        nc.sync.dma_start(q_raw0[:], qT[0].rearrange("(g r) q -> g r q", r=PACK))
        vs_pool = held.tile([P, T], F32, name="vs_pool", align_bytes=256)
        column_list = held.tile([P, PAGES * DV // GROUP], U16, name="column_list")
        nc.sync.dma_start(column_list[:], voffs)

        k_scale_pool = placed.tile([P, T // 4], I32, name="k_scale_pool", offset=K_SCALES_AT, align_bytes=256)
        nc.vector.memset(k_scale_pool[:], 0)
        nc.vector.memset(vs_pool[0:VS_ROW, :], 0.0)
        nc.sync.dma_start(k_scale_pool[0:P:SPREAD, :], k_scales[0].bitcast(I32))
        nc.sync.dma_start(vs_pool[VS_ROW : VS_ROW + 1, :], vs[0:1, :])
        k_word_pool = held.tile([P, T], I32, name="k_word_pool", align_bytes=256)
        nc.sync.dma_start(k_word_pool[:], k_words[0].rearrange("g t r -> g (t r)").bitcast(I32))

        q_bf = [reused.tile([P, NQ, PACK], BF16, name=f"q_bf{b}", tag=f"q_bf{b}", align_bytes=256) for b in range(B)]
        q_codes = [reused.tile([P, NQ], U32, name=f"q_codes{b}", tag=f"q_codes{b}", align_bytes=64) for b in range(B)]
        q_scales = [reused.tile([P, NQ], U8, name=f"q_scales{b}", tag=f"q_scales{b}", align_bytes=64) for b in range(B)]

        def cast(b, raw):
            nc.scalar.activation(q_bf[b][:], raw[:].rearrange("g r q -> g q r"), ACT.Copy)

        def quantise_queries(b):
            nc.vector.quantize_mx(out=q_codes[b][:].bitcast(FP8X4), scales=q_scales[b][:], in_=q_bf[b][:].rearrange("g q r -> g (q r)"))

        cast(0, q_raw0)
        k_scale_slots = held.tile([P, B * N // 4], I32, name="k_scale_slots", align_bytes=256)
        nc.vector.memset(k_scale_slots[:], 0)

        vs_slots = held.tile([P, PAGES * PAGE], F32, name="vs_slots")
        nc.scalar.activation(vs_slots[:], vs_pool[:].indirect(slot_list[:]), ACT.Copy)
        spread = held.tile([P, B * N], U8, name="k_scale_spread", align_bytes=64)
        nc.vector.tensor_copy(spread[:], k_scale_pool[:].bitcast(U8).indirect(slot_list[:]))
        for j in range(RUN):
            nc.sync.dma_start(k_scale_slots[j:P:QUADRANT, :], spread[:].bitcast(I32)[j * SPREAD : P : QUADRANT, :])
        q_raw1 = placed.tile([P, PACK, NQ], F32, name="q_raw1", offset=Q_RAW1_AT, align_bytes=256)
        nc.sync.dma_start(q_raw1[:], qT[1].rearrange("(g r) q -> g r q", r=PACK))
        og_sb = placed.tile([P, B, DV], F32, name="og_sb", offset=OG_AT, align_bytes=256)
        nc.sync.dma_start(og_sb[:], og.rearrange("b q e -> q b e"))
        v_scale_pool = placed.tile([P, POOL_PAGES * DV // 4], I32, name="v_scale_pool", offset=V_SCALES_AT, align_bytes=256)
        nc.vector.memset(v_scale_pool[:], 0)
        quantise_queries(0)
        cast(1, q_raw1)
        quantise_queries(1)

        v_scale_rows = v_scales.rearrange("u f e -> f u e").bitcast(I32)
        for j in range(RUN):
            nc.sync.dma_start(
                v_scale_pool[j:P:QUADRANT, :].rearrange("f (u e) -> f u e", u=POOL_PAGES), v_scale_rows[j:SCALE_ROWS:RUN, :, :]
            )
        v_word_pool = reused.tile([P, POOL_PAGES * DV], I32, name="v_word_pool", tag="q_bf0", align_bytes=256)
        nc.sync.dma_start(
            v_word_pool[:].rearrange("g (u e) -> g u e", u=POOL_PAGES),
            v_words.rearrange("u g e r -> g u (e r)").bitcast(I32),
        )

        half_tanh = held.tile([P, B * DV], F32, name="half_tanh")
        nc.scalar.activation(half_tanh[:], og_sb[:].rearrange("q b e -> q (b e)"), ACT.Tanh, scale=0.5)
        gate = held.tile([P, B * DV], F32, name="gate")
        nc.scalar.activation(gate[:], half_tanh[:], ACT.Copy, bias=0.5, scale=0.5)

        neg_scores = [reused.tile([P, PACK, P], F32, name=f"neg_scores{b}", tag=f"q_bf{b + 1}", align_bytes=256) for b in range(B)]
        first_neg_max = [held.tile([P, 1], F32, name=f"first_neg_max{b}") for b in range(B)]
        neg_max = [held.tile([P, 1], F32, name=f"neg_max{b}") for b in range(B)]
        page_sums = [held.tile([P, SEQ_PAGES], F32, name=f"page_sums{b}") for b in range(B)]
        p_sb = [held.tile([P, PACK, P], F32, name=f"p_sb{page}") for page in range(PAGES)]
        w_scales = [held.tile([P, NQ], U8, name=f"w_scales{page}", align_bytes=64) for page in range(PAGES)]
        w_codes = [held.tile([P, NQ], U32, name=f"w_codes{page}", align_bytes=64) for page in range(PAGES)]
        w_bf = [reused.tile([P, NQ, PACK], BF16, name=f"w_bf{page}", tag=f"w_bf{page}", align_bytes=64) for page in range(PAGES)]
        scores = {}
        turned = {}
        sums = {}

        def score(page):
            b = page // SEQ_PAGES
            if page == LAST:
                keys = placed.tile([P, PAGE], U32, name="k_word_slots_last", offset=Q_RAW1_AT, align_bytes=256)
            else:
                keys = reused.tile([P, PAGE], U32, name=f"k_word_slots{page}", tag=f"keys{page}", align_bytes=64)
            nc.vector.tensor_copy(keys[:], k_word_pool[:].bitcast(U32).indirect(entries(slot_list, page * PAGE, PAGE)))
            scores[page] = acc.tile([P, PAGE], F32, name="score", tag="acc")
            nc.tensor.matmul_mx(
                out=scores[page][:],
                lhsT=q_codes[b][:].bitcast(FP8X4),
                lhsT_scale=q_scales[b][:],
                rhs=keys[:].bitcast(FP8X4),
                rhs_scale=k_scale_slots[:].bitcast(U8)[:, page * PAGE : (page + 1) * PAGE],
                start=True,
                stop=True,
            )

        def dealt(page):
            return scores[page][:].rearrange("q (g r) -> q r g", r=PACK)

        def row_max(page):
            b, h = divmod(page, SEQ_PAGES)
            if h == 0:
                nc.vector.tensor_reduce(first_neg_max[b][:], scores[page][:], mybir.AxisListType.X, ALU.max, negate=True)
            else:
                nc.vector.tensor_scalar(neg_scores[b][:], dealt(page), -1.0, first_neg_max[b][:], ALU.mult, ALU.min, accum_out=neg_max[b][:])

        def exponentials(b):
            for h in range(SEQ_PAGES):
                page = b * SEQ_PAGES + h
                nc.scalar.activation(
                    p_sb[page][:],
                    neg_scores[b][:] if h else dealt(page),
                    ACT.Exp,
                    bias=neg_max[b][:],
                    scale=-1.0 if h else 1.0,
                    accum_out=page_sums[b][:, h : h + 1],
                )
                turned[page] = turn.tile([P, PACK, NQ], F32, name="turned")
                for r in range(PACK):
                    nc.tensor.transpose(turned[page][:, r, :], p_sb[page][:, r, :], ident[:])

        for page in range(LAST):
            score(page)
        ident = reused.tile([P, P], F32, name="ident", tag="keys2", align_bytes=64)
        make_identity(nc, ident[:])
        row_max(0)
        score(LAST)
        turned_tags = ("q_codes0", "q_scales0", "q_codes1", "q_scales1")
        vs_turned = [reused.tile([P, PACK], F32, name=f"vs_turned{page}", tag=turned_tags[page], align_bytes=64) for page in range(PAGES)]
        for page in range(PAGES):
            row = vs_slots[VS_ROW : VS_ROW + 1, page * PAGE : (page + 1) * PAGE]
            nc.sync.dma_start(vs_turned[page][:], row.rearrange("o (g r) -> o g r", r=PACK))
        row_max(1)
        exponentials(0)
        row_max(SEQ_PAGES)
        row_max(LAST)
        exponentials(1)

        v_scale_slots = held.tile([P, PAGES * DV], U8, name="v_scale_slots", align_bytes=64)
        nc.vector.tensor_copy(v_scale_slots[:], v_scale_pool[:].bitcast(U8).indirect(column_list[:]))
        v_word_slots = {}

        def gather_values(slots, first, count):
            nc.vector.tensor_copy(slots[:], v_word_pool[:].bitcast(U32).indirect(entries(column_list, first * DV, count * DV)))
            for e in range(count):
                v_word_slots[first + e] = slots[:, e * DV : (e + 1) * DV]

        gather_values(held.tile([P, SEQ_PAGES * DV], U32, name="v_word_slots1", align_bytes=64), SEQ_PAGES, SEQ_PAGES)

        def weigh_on_scalar(page):
            planes = reused.tile([P, PACK, NQ], BF16, name=f"planes{page}", tag=f"planes{page}", align_bytes=64)
            for r in range(PACK):
                nc.scalar.activation(planes[:, r, :], turned[page][:, r, :], ACT.Copy, scale=vs_turned[page][:, r : r + 1])
            nc.scalar.copy(
                w_bf[page][:].rearrange("g (c i) r -> g c r i", i=PACK), planes[:].rearrange("g r (c i) -> g c r i", i=PACK)
            )

        def weigh_on_vector(page):
            nc.vector.tensor_tensor(
                w_bf[page][:],
                turned[page][:].rearrange("g r q -> g q r"),
                vs_turned[page][:].unsqueeze(1).to_broadcast([P, NQ, PACK]),
                ALU.mult,
            )

        parts = (2, 1)

        def quantise(page):
            nc.vector.quantize_mx(out=w_codes[page][:].bitcast(FP8X4), scales=w_scales[page][:], in_=w_bf[page][:].rearrange("g q r -> g (q r)"))

        def multiply(page):
            b, h = divmod(page, SEQ_PAGES)
            width = DV // parts[b]
            if h == 0:
                sums[b] = [acc.tile([P, width], F32, name="sums", tag="acc") for part in range(parts[b])]
            for part in range(parts[b]):
                at = page * DV + part * width
                nc.tensor.matmul_mx(
                    out=sums[b][part][:],
                    lhsT=w_codes[page][:].bitcast(FP8X4),
                    lhsT_scale=w_scales[page][:],
                    rhs=v_word_slots[page][:, part * width : (part + 1) * width].bitcast(FP8X4),
                    rhs_scale=v_scale_slots[:, at : at + width],
                    start=h == 0,
                    stop=h == SEQ_PAGES - 1,
                )

        def finish(b):
            result = held.tile([P, DV], F32, name=f"result{b}")
            width = DV // parts[b]
            for part in range(parts[b]):
                nc.vector.scalar_tensor_tensor(
                    result[:, part * width : (part + 1) * width],
                    sums[b][part][:],
                    inverses[:, b : b + 1],
                    gate[:, b * DV + part * width : b * DV + (part + 1) * width],
                    ALU.mult,
                    ALU.mult,
                )
                nc.sync.dma_start(out[b][:, part * width : (part + 1) * width], result[:, part * width : (part + 1) * width])

        weigh_on_scalar(0)
        weigh_on_scalar(1)
        totals = reused.tile([P, B], F32, name="totals", tag="planes0", align_bytes=64)
        for b in range(B):
            nc.scalar.activation(totals[:, b : b + 1], page_sums[b][:, 0:1], ACT.Identity, bias=page_sums[b][:, 1:2], scale=1.0)
        weigh_on_vector(SEQ_PAGES)
        weigh_on_vector(LAST)
        for page in (SEQ_PAGES, LAST):
            quantise(page)
            multiply(page)
        quantise(0)
        gather_values(reused.tile([P, DV], U32, name="v_word_slots_page0", tag=turned_tags[LAST], align_bytes=64), 0, 1)
        multiply(0)
        gather_values(reused.tile([P, DV], U32, name="v_word_slots_page1", tag=f"w_bf{SEQ_PAGES}", align_bytes=64), 1, 1)
        quantise(1)
        multiply(1)
        inverses = reused.tile([P, B], F32, name="inverses", tag=turned_tags[SEQ_PAGES], align_bytes=64)
        nc.vector.reciprocal(inverses[:], totals[:])
        finish(1)
        finish(0)
